import numpy as np
import ml_dtypes


def mxq(x, axis, fmt="e4m3"):
    dtype, down = {"e4m3": (ml_dtypes.float8_e4m3fn, 7), "e5m2": (ml_dtypes.float8_e5m2, 14)}[fmt]
    v = np.moveaxis(np.asarray(x, np.float32).astype(ml_dtypes.bfloat16).astype(np.float64), axis, -1)
    blocks = v.reshape(v.shape[:-1] + (-1, 32))
    amax = np.abs(blocks).max(-1, keepdims=True)
    byte = np.maximum(np.where(amax > 0, np.frexp(amax)[1] - 1 + 127, 0) - down, 1)
    scale = np.exp2(byte - 127.0)
    codes = (blocks / scale).astype(np.float32).astype(dtype).astype(np.float64)
    return np.moveaxis((codes * scale).reshape(v.shape), -1, axis)


WIDE = False


def mx_kscale(k):
    if not WIDE:
        return np.ones(k)
    levels = np.array([10, -10, 5, -5, 0])
    if k % 512:
        return np.exp2(np.random.permutation(np.resize(levels, k // 32))).repeat(32)
    a = np.empty((k // 512, 16))
    for p in range(k // 512):
        a[p, :8] = np.random.permutation(np.resize(levels, 8))
        for g in range(8):
            far = levels[np.abs(levels - a[p, g]) >= 10]
            a[p, g + 8] = far[np.random.randint(len(far))]
    return np.exp2(a.ravel()).repeat(32)


def f64(x):
    return np.asarray(x).astype(np.float64)


def striped(idx):
    return np.tile(np.asarray(idx).reshape(-1, 16).T, (8, 1)).astype(np.uint16)


def unstriped(offs):
    return offs[:16].T.reshape(-1).astype(np.int64)


E2M1 = np.array([0.0, 0.5, 1.0, 1.5, 2.0, 3.0, 4.0, 6.0, -0.0, -0.5, -1.0, -1.5, -2.0, -3.0, -4.0, -6.0])


def pack_weight(w, fmt):
    k, n = w.shape
    w = f64(np.asarray(w, np.float32).astype(ml_dtypes.bfloat16)).reshape(k // 32, 32, n)
    amax = np.abs(w).max(1)
    if fmt == "e4m3":
        byte = np.frexp(amax)[1] - 1 + 127 - 7
    else:
        mant, ex = np.frexp(amax / 6.0)
        byte = np.where(mant > 0.5, ex, ex - 1) + 127
    byte = np.clip(np.where(amax > 0, byte, 1), 1, 254)
    scaled = (w * np.exp2(127.0 - byte)[:, None, :]).reshape(k, n).astype(np.float32)
    by_word = np.ascontiguousarray(scaled.reshape(k // 512, 128, 4, n).transpose(0, 1, 3, 2))
    if fmt == "e4m3":
        words = by_word.astype(ml_dtypes.float8_e4m3fn).view(np.uint8)
    else:
        c = by_word.astype(ml_dtypes.float4_e2m1fn).view(np.uint8) & 0xF
        words = (c[..., 0::2] | (c[..., 1::2] << 4)).reshape(k // 512, 128, 2 * n)
    return np.ascontiguousarray(words), np.ascontiguousarray(byte.astype(np.uint8).reshape(k // 512, 16, n))


def unpack_weight(words, scales, fmt):
    g, _, n = scales.shape
    words = np.ascontiguousarray(words).reshape(g, 128, n, -1)
    if fmt == "e4m3":
        vals = words.view(ml_dtypes.float8_e4m3fn).astype(np.float64)
    else:
        nib = np.empty((g, 128, n, 4), np.uint8)
        nib[..., 0::2] = words & 0xF
        nib[..., 1::2] = words >> 4
        vals = E2M1[nib]
    vals = vals * np.repeat(np.exp2(scales.astype(np.float64) - 127.0), 8, axis=1)[..., None]
    return vals.transpose(0, 1, 3, 2).reshape(g * 512, n)


B, N, T, D, NQ = 2, 512, 2048, 1024, 128


def setup_inputs():
    n = np.random.standard_normal
    seg = T // B
    idx = np.concatenate([b * seg + np.random.permutation(seg)[:N] for b in range(B)])
    s = mx_kscale(D)[:, None]
    kp = pack_weight(n((D, T)) / s, "e2m1")
    return {
        "qT": (n((B, D, NQ)) * s * (1.00 / np.sqrt(D))).astype(np.float32),
        "k_words": np.ascontiguousarray(kp[0].reshape(1, 2, 128, T, 2).transpose(0, 2, 3, 1, 4)).reshape(1, 128, T, 4),
        "k_scales": kp[1],
        "gn": (-np.log(-np.log(np.random.uniform(0.02, 0.98, (B, NQ, N))))).astype(np.float32),
        "offs": striped(idx),
    }


def reference(qT, k_words, k_scales, gn, offs):
    idx = unstriped(offs)
    pick = lambda x, which: x[:, which].reshape(x.shape[0], B, -1).transpose(1, 0, 2)
    k = unpack_weight(k_words.reshape(1, 128, T, 2, 2).transpose(0, 3, 1, 2, 4).reshape(2, 128, 2 * T), k_scales, "e2m1")
    kg = pick(k, idx)
    qq = mxq(f64(qT), 1, "e4m3")
    a = qq.transpose(0, 2, 1) @ kg
    g = 2.0 * (a + f64(gn))
    m = np.max(g, axis=-1, keepdims=True)
    e = np.exp(g - m)
    y = e / np.sum(e, axis=-1, keepdims=True)
    return y

@@ -1,0 +1,129 @@
+from contextlib import ExitStack
+
+import concourse.mybir as mybir
+
+B, N, T, D, NQ = 2, 512, 2048, 1024, 128
+FLOPS = 2 * B * NQ * N * D
+
+F32 = mybir.dt.float32
+BF16 = mybir.dt.bfloat16
+I32 = mybir.dt.int32
+U32 = mybir.dt.uint32
+U16 = mybir.dt.uint16
+U8 = mybir.dt.uint8
+FP8X4 = mybir.dt.float8_e4m3fn_x4
+FP4X4 = mybir.dt.float4_e2m1fn_x4
+ALU = mybir.AluOpType
+ACT = mybir.ActivationFunctionType
+
+P = 128
+PACK = 4
+PASSES = D // (P * PACK)
+SEG = T // B
+LIST_COLS = N // 16
+
+
+def tile_attend_gumbel_seg_kernel(tc, qT, k_words, k_scales, gn, offs, out):
+    nc = tc.nc
+    with ExitStack() as ctx:
+        keep = ctx.enter_context(tc.tile_pool(name="keep", bufs=1))
+        psum = ctx.enter_context(tc.psum_pool(name="psum", bufs=1))
+
+        offsets = keep.tile([P, B * LIST_COLS], U16, name="offsets")
+        word_pool = keep.tile([P, T], I32, name="word_pool", align_bytes=64)
+        scale_pool = keep.tile([P, T // 4], I32, name="scale_pool", align_bytes=64)
+        q_raw = [keep.tile([P, PASSES, PACK, NQ], F32, name="q_raw%d" % b, align_bytes=64) for b in range(B)]
+        noise = keep.tile([P, B, N], F32, name="noise", align_bytes=64)
+        key_scales = keep.tile([P, B * N], U8, name="key_scales", align_bytes=64)
+        moved_scales = keep.tile([P, B * N // 4], I32, name="moved_scales", align_bytes=64)
+        warm = keep.tile([P, 1], F32, name="warm")
+        warm_out = keep.tile([P, 1], F32, name="warm_out")
+
+        nc.vector.memset(scale_pool[:], 0)
+        nc.vector.memset(moved_scales[:], 0)
+        nc.gpsimd.memset(warm[:], 0.0)
+        nc.scalar.activation(warm_out[:], warm[:], ACT.Exp)
+
+        words_hbm = k_words[0].rearrange("p t c -> p (t c)").bitcast(I32)
+        scales_hbm = k_scales.bitcast(I32)
+        nc.sync.dma_start(offsets[:], offs)
+        nc.sync.dma_start(word_pool[:, 0:SEG], words_hbm[:, 0:SEG])
+        for quad in range(4):
+            nc.sync.dma_start(scale_pool[32 * quad : 32 * quad + 8, :], scales_hbm[:, 4 * quad : 4 * quad + 4, :])
+        nc.sync.dma_start(q_raw[0][:], qT[0].rearrange("(o p j) q -> p o j q", o=PASSES, j=PACK))
+        nc.sync.dma_start(word_pool[:, SEG:T], words_hbm[:, SEG:T])
+        nc.sync.dma_start(q_raw[1][:], qT[1].rearrange("(o p j) q -> p o j q", o=PASSES, j=PACK))
+        nc.sync.dma_start(noise[:], gn.rearrange("b q n -> q b n"))
+
+        pairs = [keep.tile([P, N], U32, name="pairs%d" % b, align_bytes=64) for b in range(B)]
+        key_words = [keep.tile([P, PASSES, 2 * N], U8, name="key_words%d" % b, align_bytes=64) for b in range(B)]
+        q_bf = [keep.tile([P, PASSES, NQ, PACK], BF16, name="q_bf%d" % b, align_bytes=64) for b in range(B)]
+        q_codes = [keep.tile([P, PASSES * NQ], U32, name="q_codes%d" % b, align_bytes=64) for b in range(B)]
+        q_scales = [keep.tile([P, PASSES * NQ], U8, name="q_scales%d" % b, align_bytes=64) for b in range(B)]
+        scores = [psum.tile([P, N], F32, name="scores%d" % b) for b in range(B)]
+
+        def gather_words(b):
+            window = word_pool[:, 0 : (b + 1) * SEG].bitcast(U32)
+            nc.vector.tensor_copy(pairs[b][:], window.indirect(offsets[:, b * LIST_COLS : (b + 1) * LIST_COLS]))
+
+        def part_words(b):
+            nc.vector.tensor_copy(
+                key_words[b][:].bitcast(U16),
+                pairs[b][:].bitcast(U16).rearrange("p (n o) -> p o n", o=PASSES),
+            )
+
+        def round_queries(b):
+            for o in range(PASSES):
+                nc.scalar.copy(q_bf[b][:, o, :, :], q_raw[b][:, o, :, :].rearrange("p j q -> p q j"))
+
+        def quantise_queries(b):
+            nc.vector.quantize_mx(
+                out=q_codes[b][:].bitcast(FP8X4),
+                scales=q_scales[b][:],
+                in_=q_bf[b][:].rearrange("p o q j -> p (o q j)"),
+            )
+
+        def multiply(b):
+            planes = [key_scales[:], moved_scales[:].bitcast(U8)]
+            for o in range(PASSES):
+                nc.tensor.matmul_mx(
+                    out=scores[b][:],
+                    lhsT=q_codes[b][:, o * NQ : (o + 1) * NQ].bitcast(FP8X4),
+                    lhsT_scale=q_scales[b][:, o * NQ : (o + 1) * NQ],
+                    rhs=key_words[b][:, o, :].bitcast(FP4X4),
+                    rhs_scale=planes[o][:, b * N : (b + 1) * N],
+                    start=(o == 0),
+                    stop=(o == PASSES - 1),
+                )
+
+        gather_words(0)
+        nc.vector.tensor_copy(key_scales[:], scale_pool[:].bitcast(U8).indirect(offsets[:]))
+        round_queries(0)
+        gathered = key_scales[:].bitcast(I32)
+        for j in range(4):
+            nc.scalar.dma_start(moved_scales[j:P:32, :], gathered[4 + j : P : 32, :])
+        round_queries(1)
+        part_words(0)
+        quantise_queries(0)
+        multiply(0)
+        gather_words(1)
+        part_words(1)
+        quantise_queries(1)
+        multiply(1)
+
+        noisy = [keep.tile([P, N], F32, name="noisy%d" % b, align_bytes=64) for b in range(B)]
+        neg2 = [keep.tile([P, N], F32, name="neg2_%d" % b, align_bytes=64) for b in range(B)]
+        shift = [keep.tile([P, 1], F32, name="shift%d" % b) for b in range(B)]
+        expd = [keep.tile([P, N], F32, name="expd%d" % b, align_bytes=64) for b in range(B)]
+        total = [keep.tile([P, 1], F32, name="total%d" % b) for b in range(B)]
+        inverse = [keep.tile([P, 1], F32, name="inverse%d" % b) for b in range(B)]
+        result = [keep.tile([P, N], F32, name="result%d" % b, align_bytes=64) for b in range(B)]
+
+        for b in range(B):
+            nc.vector.tensor_tensor(noisy[b][:], scores[b][:], noise[:, b, :], ALU.add)
+            nc.vector.tensor_scalar(neg2[b][:], noisy[b][:], -2.0, None, ALU.mult, ALU.min, accum_out=shift[b][:])
+            nc.scalar.activation(expd[b][:], noisy[b][:], ACT.Exp, bias=shift[b][:], scale=2.0, accum_out=total[b][:])
+        for b in range(B):
+            nc.vector.reciprocal(inverse[b][:], total[b][:])
+            nc.vector.tensor_scalar(result[b][:], expd[b][:], inverse[b][:], None, ALU.mult)
+            nc.sync.dma_start(out[b], result[b][:])

@@ -31,29 +31,28 @@ def tile_attend_gumbel_seg_kernel(tc, qT, k_words, k_scales, gn, offs, out):
 
         offsets = keep.tile([P, B * LIST_COLS], U16, name="offsets")
         word_pool = keep.tile([P, T], I32, name="word_pool", align_bytes=64)
-        scale_pool = keep.tile([P, T // 4], I32, name="scale_pool", align_bytes=64)
+        scale_pool = keep.tile([P, T // 4], I32, name="scale_pool", tag="noise", align_bytes=64)
         q_raw = [keep.tile([P, PASSES, PACK, NQ], F32, name="q_raw%d" % b, align_bytes=64) for b in range(B)]
-        noise = keep.tile([P, B, N], F32, name="noise", align_bytes=64)
         key_scales = keep.tile([P, B * N], U8, name="key_scales", align_bytes=64)
         moved_scales = keep.tile([P, B * N // 4], I32, name="moved_scales", align_bytes=64)
         warm = keep.tile([P, 1], F32, name="warm")
         warm_out = keep.tile([P, 1], F32, name="warm_out")
 
-        nc.vector.memset(scale_pool[:], 0)
-        nc.vector.memset(moved_scales[:], 0)
-        nc.gpsimd.memset(warm[:], 0.0)
-        nc.scalar.activation(warm_out[:], warm[:], ACT.Exp)
+        nc.vector.memset(warm[:], 0.0)
 
         words_hbm = k_words[0].rearrange("p t c -> p (t c)").bitcast(I32)
         scales_hbm = k_scales.bitcast(I32)
         nc.sync.dma_start(offsets[:], offs)
+        nc.sync.dma_start(scale_pool[0:32, :], scales_hbm.rearrange("o f w -> (o f) w"))
+        for quad, queue in ((1, nc.sync), (2, nc.scalar), (3, nc.scalar)):
+            rows = scales_hbm[0, 4 * quad : 4 * quad + 4, :].unsqueeze(0).broadcast_to([8, 4, T // 4])
+            queue.dma_start(scale_pool[32 * quad : 32 * quad + 32, :], rows)
+        nc.scalar.activation(warm_out[:], warm[:], ACT.Exp)
+        q_hbm = [qT[b].rearrange("(o p j) q -> p o j q", o=PASSES, j=PACK) for b in range(B)]
+        nc.sync.dma_start(q_raw[0][:], q_hbm[0])
         nc.sync.dma_start(word_pool[:, 0:SEG], words_hbm[:, 0:SEG])
-        for quad in range(4):
-            nc.sync.dma_start(scale_pool[32 * quad : 32 * quad + 8, :], scales_hbm[:, 4 * quad : 4 * quad + 4, :])
-        nc.sync.dma_start(q_raw[0][:], qT[0].rearrange("(o p j) q -> p o j q", o=PASSES, j=PACK))
+        nc.sync.dma_start(q_raw[1][:], q_hbm[1])
         nc.sync.dma_start(word_pool[:, SEG:T], words_hbm[:, SEG:T])
-        nc.sync.dma_start(q_raw[1][:], qT[1].rearrange("(o p j) q -> p o j q", o=PASSES, j=PACK))
-        nc.sync.dma_start(noise[:], gn.rearrange("b q n -> q b n"))
 
         pairs = [keep.tile([P, N], U32, name="pairs%d" % b, align_bytes=64) for b in range(B)]
         key_words = [keep.tile([P, PASSES, 2 * N], U8, name="key_words%d" % b, align_bytes=64) for b in range(B)]
@@ -66,11 +65,9 @@ def tile_attend_gumbel_seg_kernel(tc, qT, k_words, k_scales, gn, offs, out):
             window = word_pool[:, 0 : (b + 1) * SEG].bitcast(U32)
             nc.vector.tensor_copy(pairs[b][:], window.indirect(offsets[:, b * LIST_COLS : (b + 1) * LIST_COLS]))
 
-        def part_words(b):
-            nc.vector.tensor_copy(
-                key_words[b][:].bitcast(U16),
-                pairs[b][:].bitcast(U16).rearrange("p (n o) -> p o n", o=PASSES),
-            )
+        def part_words(b, passes):
+            halves = pairs[b][:].bitcast(U16).rearrange("p (n o) -> p o n", o=PASSES)
+            nc.vector.tensor_copy(key_words[b][:, passes, :].bitcast(U16), halves[:, passes, :])
 
         def round_queries(b):
             for o in range(PASSES):
@@ -96,19 +93,22 @@ def tile_attend_gumbel_seg_kernel(tc, qT, k_words, k_scales, gn, offs, out):
                     stop=(o == PASSES - 1),
                 )
 
-        gather_words(0)
         nc.vector.tensor_copy(key_scales[:], scale_pool[:].bitcast(U8).indirect(offsets[:]))
-        round_queries(0)
         gathered = key_scales[:].bitcast(I32)
-        for j in range(4):
-            nc.scalar.dma_start(moved_scales[j:P:32, :], gathered[4 + j : P : 32, :])
+        for quad in range(4):
+            nc.sync.dma_start(moved_scales[32 * quad : 32 * quad + 32, :], gathered[16 + 4 * quad : 48 + 4 * quad, :])
+        noise = keep.tile([P, B, N], F32, name="noise", tag="noise", align_bytes=64)
+        nc.sync.dma_start(noise[:], gn.rearrange("b q n -> q b n"))
+        gather_words(0)
+        round_queries(0)
         round_queries(1)
-        part_words(0)
         quantise_queries(0)
+        part_words(0, slice(0, PASSES))
         multiply(0)
         gather_words(1)
-        part_words(1)
         quantise_queries(1)
+        for o in range(PASSES):
+            part_words(1, slice(o, o + 1))
         multiply(1)
 
         noisy = [keep.tile([P, N], F32, name="noisy%d" % b, align_bytes=64) for b in range(B)]
@@ -125,5 +125,9 @@ def tile_attend_gumbel_seg_kernel(tc, qT, k_words, k_scales, gn, offs, out):
             nc.scalar.activation(expd[b][:], noisy[b][:], ACT.Exp, bias=shift[b][:], scale=2.0, accum_out=total[b][:])
         for b in range(B):
             nc.vector.reciprocal(inverse[b][:], total[b][:])
-            nc.vector.tensor_scalar(result[b][:], expd[b][:], inverse[b][:], None, ALU.mult)
-            nc.sync.dma_start(out[b], result[b][:])
+            queues = [nc.sync, nc.scalar] if b == B - 1 else [nc.sync]
+            width = N // len(queues)
+            for part, queue in enumerate(queues):
+                cols = slice(part * width, (part + 1) * width)
+                nc.vector.tensor_scalar(result[b][:, cols], expd[b][:, cols], inverse[b][:], None, ALU.mult)
+                queue.dma_start(out[b, :, cols], result[b][:, cols])

@@ -34,19 +34,20 @@ def tile_attend_gumbel_seg_kernel(tc, qT, k_words, k_scales, gn, offs, out):
         scale_pool = keep.tile([P, T // 4], I32, name="scale_pool", tag="noise", align_bytes=64)
         q_raw = [keep.tile([P, PASSES, PACK, NQ], F32, name="q_raw%d" % b, align_bytes=64) for b in range(B)]
         key_scales = keep.tile([P, B * N], U8, name="key_scales", align_bytes=64)
-        moved_scales = keep.tile([P, B * N // 4], I32, name="moved_scales", align_bytes=64)
+        moved_scales = keep.tile([P, PASSES, B * N // 4], I32, name="moved_scales", align_bytes=64)
         warm = keep.tile([P, 1], F32, name="warm")
         warm_out = keep.tile([P, 1], F32, name="warm_out")
 
+        nc.vector.memset(scale_pool[0:32, :], 0)
+        nc.vector.memset(scale_pool[96:128, :], 0)
         nc.vector.memset(warm[:], 0.0)
 
         words_hbm = k_words[0].rearrange("p t c -> p (t c)").bitcast(I32)
         scales_hbm = k_scales.bitcast(I32)
         nc.sync.dma_start(offsets[:], offs)
-        nc.sync.dma_start(scale_pool[0:32, :], scales_hbm.rearrange("o f w -> (o f) w"))
-        for quad, queue in ((1, nc.sync), (2, nc.scalar), (3, nc.scalar)):
-            rows = scales_hbm[0, 4 * quad : 4 * quad + 4, :].unsqueeze(0).broadcast_to([8, 4, T // 4])
-            queue.dma_start(scale_pool[32 * quad : 32 * quad + 32, :], rows)
+        scale_rows = scales_hbm.rearrange("o f w -> (o f) w")
+        for first_partition, first_row, queue in ((32, 0, nc.sync), (64, 4, nc.scalar), (48, 12, nc.sync), (80, 16, nc.scalar)):
+            queue.dma_start(scale_pool[first_partition : first_partition + 16, :], scale_rows[first_row : first_row + 16, :])
         nc.scalar.activation(warm_out[:], warm[:], ACT.Exp)
         q_hbm = [qT[b].rearrange("(o p j) q -> p o j q", o=PASSES, j=PACK) for b in range(B)]
         nc.sync.dma_start(q_raw[0][:], q_hbm[0])
@@ -81,22 +82,21 @@ def tile_attend_gumbel_seg_kernel(tc, qT, k_words, k_scales, gn, offs, out):
             )
 
         def multiply(b):
-            planes = [key_scales[:], moved_scales[:].bitcast(U8)]
             for o in range(PASSES):
                 nc.tensor.matmul_mx(
                     out=scores[b][:],
                     lhsT=q_codes[b][:, o * NQ : (o + 1) * NQ].bitcast(FP8X4),
                     lhsT_scale=q_scales[b][:, o * NQ : (o + 1) * NQ],
                     rhs=key_words[b][:, o, :].bitcast(FP4X4),
-                    rhs_scale=planes[o][:, b * N : (b + 1) * N],
+                    rhs_scale=moved_scales[:, o, :].bitcast(U8)[:, b * N : (b + 1) * N],
                     start=(o == 0),
                     stop=(o == PASSES - 1),
                 )
 
         nc.vector.tensor_copy(key_scales[:], scale_pool[:].bitcast(U8).indirect(offsets[:]))
         gathered = key_scales[:].bitcast(I32)
-        for quad in range(4):
-            nc.sync.dma_start(moved_scales[32 * quad : 32 * quad + 32, :], gathered[16 + 4 * quad : 48 + 4 * quad, :])
+        for o, half, source in ((0, 0, 32), (0, 1, 40), (1, 0, 52), (1, 1, 60)):
+            nc.sync.dma_start(moved_scales[64 * half : 64 * half + 64, o, :], gathered[source : source + 64, :])
         noise = keep.tile([P, B, N], F32, name="noise", tag="noise", align_bytes=64)
         nc.sync.dma_start(noise[:], gn.rearrange("b q n -> q b n"))
         gather_words(0)

@@ -46,8 +46,8 @@ def tile_attend_gumbel_seg_kernel(tc, qT, k_words, k_scales, gn, offs, out):
         scales_hbm = k_scales.bitcast(I32)
         nc.sync.dma_start(offsets[:], offs)
         scale_rows = scales_hbm.rearrange("o f w -> (o f) w")
-        for first_partition, first_row, queue in ((32, 0, nc.sync), (64, 4, nc.scalar), (48, 12, nc.sync), (80, 16, nc.scalar)):
-            queue.dma_start(scale_pool[first_partition : first_partition + 16, :], scale_rows[first_row : first_row + 16, :])
+        for first_partition, first_row, rows, queue in ((48, 0, 32, nc.scalar), (32, 12, 16, nc.sync), (80, 4, 16, nc.scalar)):
+            queue.dma_start(scale_pool[first_partition : first_partition + rows, :], scale_rows[first_row : first_row + rows, :])
         nc.scalar.activation(warm_out[:], warm[:], ACT.Exp)
         q_hbm = [qT[b].rearrange("(o p j) q -> p o j q", o=PASSES, j=PACK) for b in range(B)]
         nc.sync.dma_start(q_raw[0][:], q_hbm[0])
@@ -95,7 +95,7 @@ def tile_attend_gumbel_seg_kernel(tc, qT, k_words, k_scales, gn, offs, out):
 
         nc.vector.tensor_copy(key_scales[:], scale_pool[:].bitcast(U8).indirect(offsets[:]))
         gathered = key_scales[:].bitcast(I32)
-        for o, half, source in ((0, 0, 32), (0, 1, 40), (1, 0, 52), (1, 1, 60)):
+        for o, half, source in ((1, 0, 36), (1, 1, 44), (0, 0, 48), (0, 1, 56)):
             nc.sync.dma_start(moved_scales[64 * half : 64 * half + 64, o, :], gathered[source : source + 64, :])
         noise = keep.tile([P, B, N], F32, name="noise", tag="noise", align_bytes=64)
         nc.sync.dma_start(noise[:], gn.rearrange("b q n -> q b n"))

@@ -38,16 +38,14 @@ def tile_attend_gumbel_seg_kernel(tc, qT, k_words, k_scales, gn, offs, out):
         warm = keep.tile([P, 1], F32, name="warm")
         warm_out = keep.tile([P, 1], F32, name="warm_out")
 
-        nc.vector.memset(scale_pool[0:32, :], 0)
-        nc.vector.memset(scale_pool[96:128, :], 0)
+        nc.vector.memset(scale_pool[0:96, :], 0)
+        nc.vector.memset(moved_scales[:], 0)
         nc.vector.memset(warm[:], 0.0)
 
         words_hbm = k_words[0].rearrange("p t c -> p (t c)").bitcast(I32)
         scales_hbm = k_scales.bitcast(I32)
         nc.sync.dma_start(offsets[:], offs)
-        scale_rows = scales_hbm.rearrange("o f w -> (o f) w")
-        for first_partition, first_row, rows, queue in ((48, 0, 32, nc.scalar), (32, 12, 16, nc.sync), (80, 4, 16, nc.scalar)):
-            queue.dma_start(scale_pool[first_partition : first_partition + rows, :], scale_rows[first_row : first_row + rows, :])
+        nc.scalar.dma_start(scale_pool[96:128, :], scales_hbm.rearrange("o f w -> f o w"))
         nc.scalar.activation(warm_out[:], warm[:], ACT.Exp)
         q_hbm = [qT[b].rearrange("(o p j) q -> p o j q", o=PASSES, j=PACK) for b in range(B)]
         nc.sync.dma_start(q_raw[0][:], q_hbm[0])
@@ -95,8 +93,8 @@ def tile_attend_gumbel_seg_kernel(tc, qT, k_words, k_scales, gn, offs, out):
 
         nc.vector.tensor_copy(key_scales[:], scale_pool[:].bitcast(U8).indirect(offsets[:]))
         gathered = key_scales[:].bitcast(I32)
-        for o, half, source in ((1, 0, 36), (1, 1, 44), (0, 0, 48), (0, 1, 56)):
-            nc.sync.dma_start(moved_scales[64 * half : 64 * half + 64, o, :], gathered[source : source + 64, :])
+        for quadrant in range(4):
+            nc.sync.dma_start(moved_scales[32 * quadrant : 32 * quadrant + 4, :, :], gathered[96 + 8 * quadrant : 104 + 8 * quadrant, :])
         noise = keep.tile([P, B, N], F32, name="noise", tag="noise", align_bytes=64)
         nc.sync.dma_start(noise[:], gn.rearrange("b q n -> q b n"))
         gather_words(0)
@@ -122,7 +120,7 @@ def tile_attend_gumbel_seg_kernel(tc, qT, k_words, k_scales, gn, offs, out):
         for b in range(B):
             nc.vector.tensor_tensor(noisy[b][:], scores[b][:], noise[:, b, :], ALU.add)
             nc.vector.tensor_scalar(neg2[b][:], noisy[b][:], -2.0, None, ALU.mult, ALU.min, accum_out=shift[b][:])
-            nc.scalar.activation(expd[b][:], noisy[b][:], ACT.Exp, bias=shift[b][:], scale=2.0, accum_out=total[b][:])
+            nc.scalar.activation(expd[b][:], neg2[b][:], ACT.Exp, bias=shift[b][:], scale=-1.0, accum_out=total[b][:])
         for b in range(B):
             nc.vector.reciprocal(inverse[b][:], total[b][:])
             queues = [nc.sync, nc.scalar] if b == B - 1 else [nc.sync]

@@ -31,8 +31,7 @@ def tile_attend_gumbel_seg_kernel(tc, qT, k_words, k_scales, gn, offs, out):
 
         offsets = keep.tile([P, B * LIST_COLS], U16, name="offsets")
         word_pool = keep.tile([P, T], I32, name="word_pool", align_bytes=64)
-        scale_pool = keep.tile([P, T // 4], I32, name="scale_pool", tag="noise", align_bytes=64)
-        q_raw = [keep.tile([P, PASSES, PACK, NQ], F32, name="q_raw%d" % b, align_bytes=64) for b in range(B)]
+        scale_pool = keep.tile([P, T // 4], I32, name="scale_pool", tag="late", align_bytes=64)
         key_scales = keep.tile([P, B * N], U8, name="key_scales", align_bytes=64)
         moved_scales = keep.tile([P, PASSES, B * N // 4], I32, name="moved_scales", align_bytes=64)
         warm = keep.tile([P, 1], F32, name="warm")
@@ -44,17 +43,23 @@ def tile_attend_gumbel_seg_kernel(tc, qT, k_words, k_scales, gn, offs, out):
 
         words_hbm = k_words[0].rearrange("p t c -> p (t c)").bitcast(I32)
         scales_hbm = k_scales.bitcast(I32)
+        nc.sync.dma_start(scale_pool[96:128, :], scales_hbm.rearrange("o f w -> f o w"))
         nc.sync.dma_start(offsets[:], offs)
-        nc.scalar.dma_start(scale_pool[96:128, :], scales_hbm.rearrange("o f w -> f o w"))
         nc.scalar.activation(warm_out[:], warm[:], ACT.Exp)
-        q_hbm = [qT[b].rearrange("(o p j) q -> p o j q", o=PASSES, j=PACK) for b in range(B)]
-        nc.sync.dma_start(q_raw[0][:], q_hbm[0])
+        q_raw = {}
+
+        def load_queries(b, o, tag):
+            q_raw[b, o] = keep.tile([P, PACK, NQ], F32, name="q_raw%d_%d" % (b, o), tag=tag, align_bytes=64)
+            nc.sync.dma_start(q_raw[b, o][:], qT[b].rearrange("(o p j) q -> o p j q", o=PASSES, j=PACK)[o])
+
         nc.sync.dma_start(word_pool[:, 0:SEG], words_hbm[:, 0:SEG])
-        nc.sync.dma_start(q_raw[1][:], q_hbm[1])
+        load_queries(0, 0, "noise")
+        load_queries(0, 1, "keys0")
         nc.sync.dma_start(word_pool[:, SEG:T], words_hbm[:, SEG:T])
+        load_queries(1, 0, "keys1")
 
         pairs = [keep.tile([P, N], U32, name="pairs%d" % b, align_bytes=64) for b in range(B)]
-        key_words = [keep.tile([P, PASSES, 2 * N], U8, name="key_words%d" % b, align_bytes=64) for b in range(B)]
+        key_words = [keep.tile([P, PASSES, 2 * N], U8, name="key_words%d" % b, tag="keys%d" % b, align_bytes=64) for b in range(B)]
         q_bf = [keep.tile([P, PASSES, NQ, PACK], BF16, name="q_bf%d" % b, align_bytes=64) for b in range(B)]
         q_codes = [keep.tile([P, PASSES * NQ], U32, name="q_codes%d" % b, align_bytes=64) for b in range(B)]
         q_scales = [keep.tile([P, PASSES * NQ], U8, name="q_scales%d" % b, align_bytes=64) for b in range(B)]
@@ -70,13 +75,14 @@ def tile_attend_gumbel_seg_kernel(tc, qT, k_words, k_scales, gn, offs, out):
 
         def round_queries(b):
             for o in range(PASSES):
-                nc.scalar.copy(q_bf[b][:, o, :, :], q_raw[b][:, o, :, :].rearrange("p j q -> p q j"))
+                nc.scalar.copy(q_bf[b][:, o, :, :], q_raw[b, o][:].rearrange("p j q -> p q j"))
 
-        def quantise_queries(b):
+        def quantise_queries(b, passes):
+            cols = slice(passes.start * NQ, passes.stop * NQ)
             nc.vector.quantize_mx(
-                out=q_codes[b][:].bitcast(FP8X4),
-                scales=q_scales[b][:],
-                in_=q_bf[b][:].rearrange("p o q j -> p (o q j)"),
+                out=q_codes[b][:, cols].bitcast(FP8X4),
+                scales=q_scales[b][:, cols],
+                in_=q_bf[b][:, passes, :, :].rearrange("p o q j -> p (o q j)"),
             )
 
         def multiply(b):
@@ -95,21 +101,24 @@ def tile_attend_gumbel_seg_kernel(tc, qT, k_words, k_scales, gn, offs, out):
         gathered = key_scales[:].bitcast(I32)
         for quadrant in range(4):
             nc.sync.dma_start(moved_scales[32 * quadrant : 32 * quadrant + 4, :, :], gathered[96 + 8 * quadrant : 104 + 8 * quadrant, :])
-        noise = keep.tile([P, B, N], F32, name="noise", tag="noise", align_bytes=64)
-        nc.sync.dma_start(noise[:], gn.rearrange("b q n -> q b n"))
+        load_queries(1, 1, "late")
         gather_words(0)
         round_queries(0)
+        noise = keep.tile([P, B, N], F32, name="noise", tag="noise", align_bytes=64)
+        for b in range(B):
+            nc.sync.dma_start(noise[:, b, :], gn[b])
         round_queries(1)
-        quantise_queries(0)
+        quantise_queries(0, slice(0, PASSES))
         part_words(0, slice(0, PASSES))
         multiply(0)
         gather_words(1)
-        quantise_queries(1)
+        quantise_queries(1, slice(0, 1))
         for o in range(PASSES):
             part_words(1, slice(o, o + 1))
+        quantise_queries(1, slice(1, 2))
         multiply(1)
 
-        noisy = [keep.tile([P, N], F32, name="noisy%d" % b, align_bytes=64) for b in range(B)]
+        noisy = [keep.tile([P, N], F32, name="noisy%d" % b, tag="late" if b == 0 else "noisy", align_bytes=64) for b in range(B)]
         neg2 = [keep.tile([P, N], F32, name="neg2_%d" % b, align_bytes=64) for b in range(B)]
         shift = [keep.tile([P, 1], F32, name="shift%d" % b) for b in range(B)]
         expd = [keep.tile([P, N], F32, name="expd%d" % b, align_bytes=64) for b in range(B)]

@@ -21,12 +21,14 @@ PACK = 4
 PASSES = D // (P * PACK)
 SEG = T // B
 LIST_COLS = N // 16
+HALF = N // 2
 
 
 def tile_attend_gumbel_seg_kernel(tc, qT, k_words, k_scales, gn, offs, out):
     nc = tc.nc
     with ExitStack() as ctx:
         keep = ctx.enter_context(tc.tile_pool(name="keep", bufs=1))
+        shared = ctx.enter_context(tc.tile_pool(name="shared", bufs=1))
         psum = ctx.enter_context(tc.psum_pool(name="psum", bufs=1))
 
         offsets = keep.tile([P, B * LIST_COLS], U16, name="offsets")
@@ -34,48 +36,55 @@ def tile_attend_gumbel_seg_kernel(tc, qT, k_words, k_scales, gn, offs, out):
         scale_pool = keep.tile([P, T // 4], I32, name="scale_pool", tag="late", align_bytes=64)
         key_scales = keep.tile([P, B * N], U8, name="key_scales", align_bytes=64)
         moved_scales = keep.tile([P, PASSES, B * N // 4], I32, name="moved_scales", align_bytes=64)
-        warm = keep.tile([P, 1], F32, name="warm")
-        warm_out = keep.tile([P, 1], F32, name="warm_out")
 
         nc.vector.memset(scale_pool[0:96, :], 0)
         nc.vector.memset(moved_scales[:], 0)
-        nc.vector.memset(warm[:], 0.0)
 
         words_hbm = k_words[0].rearrange("p t c -> p (t c)").bitcast(I32)
         scales_hbm = k_scales.bitcast(I32)
         nc.sync.dma_start(scale_pool[96:128, :], scales_hbm.rearrange("o f w -> f o w"))
         nc.sync.dma_start(offsets[:], offs)
-        nc.scalar.activation(warm_out[:], warm[:], ACT.Exp)
         q_raw = {}
 
-        def load_queries(b, o, tag):
-            q_raw[b, o] = keep.tile([P, PACK, NQ], F32, name="q_raw%d_%d" % (b, o), tag=tag, align_bytes=64)
+        def load_queries(b, o, tile):
+            q_raw[b, o] = tile
             nc.sync.dma_start(q_raw[b, o][:], qT[b].rearrange("(o p j) q -> o p j q", o=PASSES, j=PACK)[o])
 
         nc.sync.dma_start(word_pool[:, 0:SEG], words_hbm[:, 0:SEG])
-        load_queries(0, 0, "noise")
-        load_queries(0, 1, "keys0")
+        load_queries(0, 0, keep.tile([P, PACK, NQ], F32, name="q_raw0_0", tag="noise", align_bytes=64))
+        load_queries(0, 1, shared.tile([P, PACK, NQ], F32, name="q_raw0_1", offset=1024, align_bytes=64))
         nc.sync.dma_start(word_pool[:, SEG:T], words_hbm[:, SEG:T])
-        load_queries(1, 0, "keys1")
+        load_queries(1, 0, keep.tile([P, PACK, NQ], F32, name="q_raw1_0", tag="keys1", align_bytes=64))
 
-        pairs = [keep.tile([P, N], U32, name="pairs%d" % b, align_bytes=64) for b in range(B)]
-        key_words = [keep.tile([P, PASSES, 2 * N], U8, name="key_words%d" % b, tag="keys%d" % b, align_bytes=64) for b in range(B)]
+        pairs = [
+            keep.tile([P, N], U32, name="pairs0", align_bytes=64),
+            shared.tile([P, N], U32, name="pairs1", offset=2048, align_bytes=64),
+        ]
+        key_words = [
+            shared.tile([P, PASSES, 2 * N], U8, name="key_words0", offset=0, align_bytes=64),
+            keep.tile([P, PASSES, 2 * N], U8, name="key_words1", tag="keys1", align_bytes=64),
+        ]
         q_bf = [keep.tile([P, PASSES, NQ, PACK], BF16, name="q_bf%d" % b, align_bytes=64) for b in range(B)]
         q_codes = [keep.tile([P, PASSES * NQ], U32, name="q_codes%d" % b, align_bytes=64) for b in range(B)]
         q_scales = [keep.tile([P, PASSES * NQ], U8, name="q_scales%d" % b, align_bytes=64) for b in range(B)]
-        scores = [psum.tile([P, N], F32, name="scores%d" % b) for b in range(B)]
+        first_scores = psum.tile([P, N], F32, name="first_scores")
+        last_scores = [psum.tile([P, HALF], F32, name="last_scores%d" % h) for h in range(2)]
 
-        def gather_words(b):
+        def gather_words(b, slots):
             window = word_pool[:, 0 : (b + 1) * SEG].bitcast(U32)
-            nc.vector.tensor_copy(pairs[b][:], window.indirect(offsets[:, b * LIST_COLS : (b + 1) * LIST_COLS]))
+            entries = offsets[:, b * LIST_COLS + slots.start // 16 : b * LIST_COLS + slots.stop // 16]
+            nc.vector.tensor_copy(pairs[b][:, slots], window.indirect(entries))
 
-        def part_words(b, passes):
+        def part_words(b, slots):
             halves = pairs[b][:].bitcast(U16).rearrange("p (n o) -> p o n", o=PASSES)
-            nc.vector.tensor_copy(key_words[b][:, passes, :].bitcast(U16), halves[:, passes, :])
+            nc.vector.tensor_copy(key_words[b][:].bitcast(U16)[:, :, slots], halves[:, :, slots])
 
         def round_queries(b):
             for o in range(PASSES):
-                nc.scalar.copy(q_bf[b][:, o, :, :], q_raw[b, o][:].rearrange("p j q -> p q j"))
+                nc.scalar.copy(
+                    q_bf[b][:, o, :, :].rearrange("p (c i) j -> p c j i", i=4),
+                    q_raw[b, o][:].rearrange("p j (c i) -> p c j i", i=4),
+                )
 
         def quantise_queries(b, passes):
             cols = slice(passes.start * NQ, passes.stop * NQ)
@@ -85,14 +94,14 @@ def tile_attend_gumbel_seg_kernel(tc, qT, k_words, k_scales, gn, offs, out):
                 in_=q_bf[b][:, passes, :, :].rearrange("p o q j -> p (o q j)"),
             )
 
-        def multiply(b):
+        def multiply(b, first_slot, width, scores):
             for o in range(PASSES):
                 nc.tensor.matmul_mx(
-                    out=scores[b][:],
+                    out=scores,
                     lhsT=q_codes[b][:, o * NQ : (o + 1) * NQ].bitcast(FP8X4),
                     lhsT_scale=q_scales[b][:, o * NQ : (o + 1) * NQ],
-                    rhs=key_words[b][:, o, :].bitcast(FP4X4),
-                    rhs_scale=moved_scales[:, o, :].bitcast(U8)[:, b * N : (b + 1) * N],
+                    rhs=key_words[b][:, o, 2 * first_slot : 2 * (first_slot + width)].bitcast(FP4X4),
+                    rhs_scale=moved_scales[:, o, :].bitcast(U8)[:, b * N + first_slot : b * N + first_slot + width],
                     start=(o == 0),
                     stop=(o == PASSES - 1),
                 )
@@ -101,22 +110,23 @@ def tile_attend_gumbel_seg_kernel(tc, qT, k_words, k_scales, gn, offs, out):
         gathered = key_scales[:].bitcast(I32)
         for quadrant in range(4):
             nc.sync.dma_start(moved_scales[32 * quadrant : 32 * quadrant + 4, :, :], gathered[96 + 8 * quadrant : 104 + 8 * quadrant, :])
-        load_queries(1, 1, "late")
-        gather_words(0)
+        load_queries(1, 1, keep.tile([P, PACK, NQ], F32, name="q_raw1_1", tag="late", align_bytes=64))
+        gather_words(0, slice(0, N))
         round_queries(0)
         noise = keep.tile([P, B, N], F32, name="noise", tag="noise", align_bytes=64)
         for b in range(B):
             nc.sync.dma_start(noise[:, b, :], gn[b])
         round_queries(1)
         quantise_queries(0, slice(0, PASSES))
-        part_words(0, slice(0, PASSES))
-        multiply(0)
-        gather_words(1)
-        quantise_queries(1, slice(0, 1))
-        for o in range(PASSES):
-            part_words(1, slice(o, o + 1))
-        quantise_queries(1, slice(1, 2))
-        multiply(1)
+        part_words(0, slice(0, N))
+        multiply(0, 0, N, first_scores[:])
+        for h in range(2):
+            gather_words(1, slice(h * HALF, (h + 1) * HALF))
+            quantise_queries(1, slice(h, h + 1))
+            part_words(1, slice(h * HALF, (h + 1) * HALF))
+        for h in range(2):
+            for first_slot in (0, P):
+                multiply(1, h * HALF + first_slot, P, last_scores[h][:, first_slot : first_slot + P])
 
         noisy = [keep.tile([P, N], F32, name="noisy%d" % b, tag="late" if b == 0 else "noisy", align_bytes=64) for b in range(B)]
         neg2 = [keep.tile([P, N], F32, name="neg2_%d" % b, align_bytes=64) for b in range(B)]
@@ -126,10 +136,15 @@ def tile_attend_gumbel_seg_kernel(tc, qT, k_words, k_scales, gn, offs, out):
         inverse = [keep.tile([P, 1], F32, name="inverse%d" % b) for b in range(B)]
         result = [keep.tile([P, N], F32, name="result%d" % b, align_bytes=64) for b in range(B)]
 
-        for b in range(B):
-            nc.vector.tensor_tensor(noisy[b][:], scores[b][:], noise[:, b, :], ALU.add)
+        def exponentials(b):
             nc.vector.tensor_scalar(neg2[b][:], noisy[b][:], -2.0, None, ALU.mult, ALU.min, accum_out=shift[b][:])
             nc.scalar.activation(expd[b][:], neg2[b][:], ACT.Exp, bias=shift[b][:], scale=-1.0, accum_out=total[b][:])
+
+        nc.vector.tensor_tensor(noisy[0][:], first_scores[:], noise[:, 0, :], ALU.add)
+        nc.vector.tensor_tensor(noisy[1][:, 0:HALF], last_scores[0][:], noise[:, 1, 0:HALF], ALU.add)
+        nc.vector.tensor_tensor(noisy[1][:, HALF:N], last_scores[1][:], noise[:, 1, HALF:N], ALU.add)
+        exponentials(0)
+        exponentials(1)
         for b in range(B):
             nc.vector.reciprocal(inverse[b][:], total[b][:])
             queues = [nc.sync, nc.scalar] if b == B - 1 else [nc.sync]

@@ -29,6 +29,7 @@ def tile_attend_gumbel_seg_kernel(tc, qT, k_words, k_scales, gn, offs, out):
     with ExitStack() as ctx:
         keep = ctx.enter_context(tc.tile_pool(name="keep", bufs=1))
         shared = ctx.enter_context(tc.tile_pool(name="shared", bufs=1))
+        third = ctx.enter_context(tc.tile_pool(name="third", bufs=1))
         psum = ctx.enter_context(tc.psum_pool(name="psum", bufs=1))
 
         offsets = keep.tile([P, B * LIST_COLS], U16, name="offsets")
@@ -54,30 +55,30 @@ def tile_attend_gumbel_seg_kernel(tc, qT, k_words, k_scales, gn, offs, out):
         load_queries(0, 0, keep.tile([P, PACK, NQ], F32, name="q_raw0_0", tag="noise", align_bytes=64))
         load_queries(0, 1, shared.tile([P, PACK, NQ], F32, name="q_raw0_1", offset=1024, align_bytes=64))
         nc.sync.dma_start(word_pool[:, SEG:T], words_hbm[:, SEG:T])
-        load_queries(1, 0, keep.tile([P, PACK, NQ], F32, name="q_raw1_0", tag="keys1", align_bytes=64))
+        load_queries(1, 0, third.tile([P, PACK, NQ], F32, name="q_raw1_0", offset=0, align_bytes=64))
 
         pairs = [
             keep.tile([P, N], U32, name="pairs0", align_bytes=64),
             shared.tile([P, N], U32, name="pairs1", offset=2048, align_bytes=64),
         ]
-        key_words = [
-            shared.tile([P, PASSES, 2 * N], U8, name="key_words0", offset=0, align_bytes=64),
-            keep.tile([P, PASSES, 2 * N], U8, name="key_words1", tag="keys1", align_bytes=64),
-        ]
+        first_keys = shared.tile([P, PASSES, 2 * N], U8, name="first_keys", offset=0, align_bytes=64)
+        last_keys = [third.tile([P, 2 * N], U8, name="last_keys%d" % o, offset=2 * N * o, align_bytes=64) for o in range(PASSES)]
+        key_words = {}
+        for o in range(PASSES):
+            key_words[0, o] = first_keys[:, o, :]
+            key_words[1, o] = last_keys[o][:]
         q_bf = [keep.tile([P, PASSES, NQ, PACK], BF16, name="q_bf%d" % b, align_bytes=64) for b in range(B)]
         q_codes = [keep.tile([P, PASSES * NQ], U32, name="q_codes%d" % b, align_bytes=64) for b in range(B)]
         q_scales = [keep.tile([P, PASSES * NQ], U8, name="q_scales%d" % b, align_bytes=64) for b in range(B)]
         first_scores = psum.tile([P, N], F32, name="first_scores")
-        last_scores = [psum.tile([P, HALF], F32, name="last_scores%d" % h) for h in range(2)]
+        last_scores = psum.tile([P, N], F32, name="last_scores")
 
         def gather_words(b, slots):
             window = word_pool[:, 0 : (b + 1) * SEG].bitcast(U32)
             entries = offsets[:, b * LIST_COLS + slots.start // 16 : b * LIST_COLS + slots.stop // 16]
             nc.vector.tensor_copy(pairs[b][:, slots], window.indirect(entries))
 
-        def part_words(b, slots):
-            halves = pairs[b][:].bitcast(U16).rearrange("p (n o) -> p o n", o=PASSES)
-            nc.vector.tensor_copy(key_words[b][:].bitcast(U16)[:, :, slots], halves[:, :, slots])
+        by_pass = [pairs[b][:].bitcast(U16).rearrange("p (n o) -> p o n", o=PASSES) for b in range(B)]
 
         def round_queries(b):
             for o in range(PASSES):
@@ -100,7 +101,7 @@ def tile_attend_gumbel_seg_kernel(tc, qT, k_words, k_scales, gn, offs, out):
                     out=scores,
                     lhsT=q_codes[b][:, o * NQ : (o + 1) * NQ].bitcast(FP8X4),
                     lhsT_scale=q_scales[b][:, o * NQ : (o + 1) * NQ],
-                    rhs=key_words[b][:, o, 2 * first_slot : 2 * (first_slot + width)].bitcast(FP4X4),
+                    rhs=key_words[b, o][:, 2 * first_slot : 2 * (first_slot + width)].bitcast(FP4X4),
                     rhs_scale=moved_scales[:, o, :].bitcast(U8)[:, b * N + first_slot : b * N + first_slot + width],
                     start=(o == 0),
                     stop=(o == PASSES - 1),
@@ -118,32 +119,37 @@ def tile_attend_gumbel_seg_kernel(tc, qT, k_words, k_scales, gn, offs, out):
             nc.sync.dma_start(noise[:, b, :], gn[b])
         round_queries(1)
         quantise_queries(0, slice(0, PASSES))
-        part_words(0, slice(0, N))
+        nc.vector.tensor_copy(first_keys[:].bitcast(U16), by_pass[0])
         multiply(0, 0, N, first_scores[:])
-        for h in range(2):
-            gather_words(1, slice(h * HALF, (h + 1) * HALF))
-            quantise_queries(1, slice(h, h + 1))
-            part_words(1, slice(h * HALF, (h + 1) * HALF))
-        for h in range(2):
-            for first_slot in (0, P):
-                multiply(1, h * HALF + first_slot, P, last_scores[h][:, first_slot : first_slot + P])
+        gather_words(1, slice(0, N))
+        quantise_queries(1, slice(0, 1))
+        for o in range(PASSES):
+            nc.vector.tensor_copy(last_keys[o][:].bitcast(U16), by_pass[1][:, o, :])
+        quantise_queries(1, slice(1, 2))
+        multiply(1, 0, N, last_scores[:])
 
         noisy = [keep.tile([P, N], F32, name="noisy%d" % b, tag="late" if b == 0 else "noisy", align_bytes=64) for b in range(B)]
         neg2 = [keep.tile([P, N], F32, name="neg2_%d" % b, align_bytes=64) for b in range(B)]
-        shift = [keep.tile([P, 1], F32, name="shift%d" % b) for b in range(B)]
+        part_shift = keep.tile([P, 1], F32, name="part_shift")
+        shift = [third.tile([P, 1], F32, name="shift0", offset=2 * N, align_bytes=64), keep.tile([P, 1], F32, name="shift1")]
         expd = [keep.tile([P, N], F32, name="expd%d" % b, align_bytes=64) for b in range(B)]
         total = [keep.tile([P, 1], F32, name="total%d" % b) for b in range(B)]
         inverse = [keep.tile([P, 1], F32, name="inverse%d" % b) for b in range(B)]
         result = [keep.tile([P, N], F32, name="result%d" % b, align_bytes=64) for b in range(B)]
 
+        def row_minimum(b, cols, start, target):
+            nc.vector.tensor_scalar(neg2[b][:, cols], noisy[b][:, cols], -2.0, start, ALU.mult, ALU.min, accum_out=target)
+
         def exponentials(b):
-            nc.vector.tensor_scalar(neg2[b][:], noisy[b][:], -2.0, None, ALU.mult, ALU.min, accum_out=shift[b][:])
             nc.scalar.activation(expd[b][:], neg2[b][:], ACT.Exp, bias=shift[b][:], scale=-1.0, accum_out=total[b][:])
 
-        nc.vector.tensor_tensor(noisy[0][:], first_scores[:], noise[:, 0, :], ALU.add)
-        nc.vector.tensor_tensor(noisy[1][:, 0:HALF], last_scores[0][:], noise[:, 1, 0:HALF], ALU.add)
-        nc.vector.tensor_tensor(noisy[1][:, HALF:N], last_scores[1][:], noise[:, 1, HALF:N], ALU.add)
+        for cols in (slice(0, HALF), slice(HALF, N)):
+            nc.vector.tensor_tensor(noisy[0][:, cols], first_scores[:, cols], noise[:, 0, cols], ALU.add)
+        row_minimum(0, slice(0, HALF), None, part_shift[:])
+        nc.vector.tensor_tensor(noisy[1][:], last_scores[:], noise[:, 1, :], ALU.add)
+        row_minimum(0, slice(HALF, N), part_shift[:], shift[0][:])
         exponentials(0)
+        row_minimum(1, slice(0, N), None, shift[1][:])
         exponentials(1)
         for b in range(B):
             nc.vector.reciprocal(inverse[b][:], total[b][:])

@@ -21,7 +21,12 @@ PACK = 4
 PASSES = D // (P * PACK)
 SEG = T // B
 LIST_COLS = N // 16
-HALF = N // 2
+QUADRANT = 32
+QUADRANTS = P // QUADRANT
+BLOCK_ROWS = 4
+SCALE_BASE = P - QUADRANT
+PASS_BYTES = 2 * N
+EARLY = 384
 
 
 def tile_attend_gumbel_seg_kernel(tc, qT, k_words, k_scales, gn, offs, out):
@@ -38,12 +43,12 @@ def tile_attend_gumbel_seg_kernel(tc, qT, k_words, k_scales, gn, offs, out):
         key_scales = keep.tile([P, B * N], U8, name="key_scales", align_bytes=64)
         moved_scales = keep.tile([P, PASSES, B * N // 4], I32, name="moved_scales", align_bytes=64)
 
-        nc.vector.memset(scale_pool[0:96, :], 0)
+        nc.vector.memset(scale_pool[0:SCALE_BASE, :], 0)
         nc.vector.memset(moved_scales[:], 0)
 
         words_hbm = k_words[0].rearrange("p t c -> p (t c)").bitcast(I32)
         scales_hbm = k_scales.bitcast(I32)
-        nc.sync.dma_start(scale_pool[96:128, :], scales_hbm.rearrange("o f w -> f o w"))
+        nc.sync.dma_start(scale_pool[SCALE_BASE:P, :], scales_hbm.rearrange("o f w -> f o w"))
         nc.sync.dma_start(offsets[:], offs)
         q_raw = {}
 
@@ -53,16 +58,16 @@ def tile_attend_gumbel_seg_kernel(tc, qT, k_words, k_scales, gn, offs, out):
 
         nc.sync.dma_start(word_pool[:, 0:SEG], words_hbm[:, 0:SEG])
         load_queries(0, 0, keep.tile([P, PACK, NQ], F32, name="q_raw0_0", tag="noise", align_bytes=64))
-        load_queries(0, 1, shared.tile([P, PACK, NQ], F32, name="q_raw0_1", offset=1024, align_bytes=64))
+        load_queries(0, 1, shared.tile([P, PACK, NQ], F32, name="q_raw0_1", offset=PASS_BYTES, align_bytes=64))
         nc.sync.dma_start(word_pool[:, SEG:T], words_hbm[:, SEG:T])
         load_queries(1, 0, third.tile([P, PACK, NQ], F32, name="q_raw1_0", offset=0, align_bytes=64))
 
         pairs = [
             keep.tile([P, N], U32, name="pairs0", align_bytes=64),
-            shared.tile([P, N], U32, name="pairs1", offset=2048, align_bytes=64),
+            shared.tile([P, N], U32, name="pairs1", offset=PASSES * PASS_BYTES, align_bytes=64),
         ]
-        first_keys = shared.tile([P, PASSES, 2 * N], U8, name="first_keys", offset=0, align_bytes=64)
-        last_keys = [third.tile([P, 2 * N], U8, name="last_keys%d" % o, offset=2 * N * o, align_bytes=64) for o in range(PASSES)]
+        first_keys = shared.tile([P, PASSES, PASS_BYTES], U8, name="first_keys", offset=0, align_bytes=64)
+        last_keys = [third.tile([P, PASS_BYTES], U8, name="last_keys%d" % o, offset=PASS_BYTES * o, align_bytes=64) for o in range(PASSES)]
         key_words = {}
         for o in range(PASSES):
             key_words[0, o] = first_keys[:, o, :]
@@ -70,15 +75,12 @@ def tile_attend_gumbel_seg_kernel(tc, qT, k_words, k_scales, gn, offs, out):
         q_bf = [keep.tile([P, PASSES, NQ, PACK], BF16, name="q_bf%d" % b, align_bytes=64) for b in range(B)]
         q_codes = [keep.tile([P, PASSES * NQ], U32, name="q_codes%d" % b, align_bytes=64) for b in range(B)]
         q_scales = [keep.tile([P, PASSES * NQ], U8, name="q_scales%d" % b, align_bytes=64) for b in range(B)]
-        first_scores = psum.tile([P, N], F32, name="first_scores")
-        last_scores = psum.tile([P, N], F32, name="last_scores")
-
-        def gather_words(b, slots):
-            window = word_pool[:, 0 : (b + 1) * SEG].bitcast(U32)
-            entries = offsets[:, b * LIST_COLS + slots.start // 16 : b * LIST_COLS + slots.stop // 16]
-            nc.vector.tensor_copy(pairs[b][:, slots], window.indirect(entries))
-
+        scores = [psum.tile([P, N], F32, name=name) for name in ("first_scores", "last_scores")]
         by_pass = [pairs[b][:].bitcast(U16).rearrange("p (n o) -> p o n", o=PASSES) for b in range(B)]
+
+        def gather_words(b):
+            window = word_pool[:, 0 : (b + 1) * SEG].bitcast(U32)
+            nc.vector.tensor_copy(pairs[b][:], window.indirect(offsets[:, b * LIST_COLS : (b + 1) * LIST_COLS]))
 
         def round_queries(b):
             for o in range(PASSES):
@@ -95,47 +97,57 @@ def tile_attend_gumbel_seg_kernel(tc, qT, k_words, k_scales, gn, offs, out):
                 in_=q_bf[b][:, passes, :, :].rearrange("p o q j -> p (o q j)"),
             )
 
-        def multiply(b, first_slot, width, scores):
+        def multiply(b):
             for o in range(PASSES):
                 nc.tensor.matmul_mx(
-                    out=scores,
+                    out=scores[b][:],
                     lhsT=q_codes[b][:, o * NQ : (o + 1) * NQ].bitcast(FP8X4),
                     lhsT_scale=q_scales[b][:, o * NQ : (o + 1) * NQ],
-                    rhs=key_words[b, o][:, 2 * first_slot : 2 * (first_slot + width)].bitcast(FP4X4),
-                    rhs_scale=moved_scales[:, o, :].bitcast(U8)[:, b * N + first_slot : b * N + first_slot + width],
+                    rhs=key_words[b, o].bitcast(FP4X4),
+                    rhs_scale=moved_scales[:, o, :].bitcast(U8)[:, b * N : (b + 1) * N],
                     start=(o == 0),
                     stop=(o == PASSES - 1),
                 )
 
         nc.vector.tensor_copy(key_scales[:], scale_pool[:].bitcast(U8).indirect(offsets[:]))
         gathered = key_scales[:].bitcast(I32)
-        for quadrant in range(4):
-            nc.sync.dma_start(moved_scales[32 * quadrant : 32 * quadrant + 4, :, :], gathered[96 + 8 * quadrant : 104 + 8 * quadrant, :])
+        rows_moved = BLOCK_ROWS * PASSES
+        for quadrant in range(QUADRANTS):
+            nc.sync.dma_start(
+                moved_scales[QUADRANT * quadrant : QUADRANT * quadrant + BLOCK_ROWS, :, :],
+                gathered[SCALE_BASE + rows_moved * quadrant : SCALE_BASE + rows_moved * (quadrant + 1), :],
+            )
+
         load_queries(1, 1, keep.tile([P, PACK, NQ], F32, name="q_raw1_1", tag="late", align_bytes=64))
-        gather_words(0, slice(0, N))
+        gather_words(0)
         round_queries(0)
         noise = keep.tile([P, B, N], F32, name="noise", tag="noise", align_bytes=64)
         for b in range(B):
             nc.sync.dma_start(noise[:, b, :], gn[b])
         round_queries(1)
+
         quantise_queries(0, slice(0, PASSES))
         nc.vector.tensor_copy(first_keys[:].bitcast(U16), by_pass[0])
-        multiply(0, 0, N, first_scores[:])
-        gather_words(1, slice(0, N))
+        multiply(0)
+        gather_words(1)
         quantise_queries(1, slice(0, 1))
         for o in range(PASSES):
             nc.vector.tensor_copy(last_keys[o][:].bitcast(U16), by_pass[1][:, o, :])
         quantise_queries(1, slice(1, 2))
-        multiply(1, 0, N, last_scores[:])
+        multiply(1)
 
-        noisy = [keep.tile([P, N], F32, name="noisy%d" % b, tag="late" if b == 0 else "noisy", align_bytes=64) for b in range(B)]
+        first_sums = keep.tile([P, N], F32, name="first_sums", tag="late", align_bytes=64)
+        noisy = [first_sums[:], noise[:, 0, :]]
         neg2 = [keep.tile([P, N], F32, name="neg2_%d" % b, align_bytes=64) for b in range(B)]
         part_shift = keep.tile([P, 1], F32, name="part_shift")
-        shift = [third.tile([P, 1], F32, name="shift0", offset=2 * N, align_bytes=64), keep.tile([P, 1], F32, name="shift1")]
+        shift = [third.tile([P, 1], F32, name="shift0", offset=PASS_BYTES, align_bytes=64), keep.tile([P, 1], F32, name="shift1")]
         expd = [keep.tile([P, N], F32, name="expd%d" % b, align_bytes=64) for b in range(B)]
         total = [keep.tile([P, 1], F32, name="total%d" % b) for b in range(B)]
         inverse = [keep.tile([P, 1], F32, name="inverse%d" % b) for b in range(B)]
         result = [keep.tile([P, N], F32, name="result%d" % b, align_bytes=64) for b in range(B)]
+
+        def add_noise(b, cols):
+            nc.vector.tensor_tensor(noisy[b][:, cols], scores[b][:, cols], noise[:, b, cols], ALU.add)
 
         def row_minimum(b, cols, start, target):
             nc.vector.tensor_scalar(neg2[b][:, cols], noisy[b][:, cols], -2.0, start, ALU.mult, ALU.min, accum_out=target)
@@ -143,14 +155,16 @@ def tile_attend_gumbel_seg_kernel(tc, qT, k_words, k_scales, gn, offs, out):
         def exponentials(b):
             nc.scalar.activation(expd[b][:], neg2[b][:], ACT.Exp, bias=shift[b][:], scale=-1.0, accum_out=total[b][:])
 
-        for cols in (slice(0, HALF), slice(HALF, N)):
-            nc.vector.tensor_tensor(noisy[0][:, cols], first_scores[:, cols], noise[:, 0, cols], ALU.add)
-        row_minimum(0, slice(0, HALF), None, part_shift[:])
-        nc.vector.tensor_tensor(noisy[1][:], last_scores[:], noise[:, 1, :], ALU.add)
-        row_minimum(0, slice(HALF, N), part_shift[:], shift[0][:])
+        early, late, whole = slice(0, EARLY), slice(EARLY, N), slice(0, N)
+        add_noise(0, early)
+        add_noise(0, late)
+        row_minimum(0, early, None, part_shift[:])
+        add_noise(1, whole)
+        row_minimum(0, late, part_shift[:], shift[0][:])
         exponentials(0)
-        row_minimum(1, slice(0, N), None, shift[1][:])
+        row_minimum(1, whole, None, shift[1][:])
         exponentials(1)
+
         for b in range(B):
             nc.vector.reciprocal(inverse[b][:], total[b][:])
             queues = [nc.sync, nc.scalar] if b == B - 1 else [nc.sync]

@@ -38,17 +38,17 @@ def tile_attend_gumbel_seg_kernel(tc, qT, k_words, k_scales, gn, offs, out):
         psum = ctx.enter_context(tc.psum_pool(name="psum", bufs=1))
 
         offsets = keep.tile([P, B * LIST_COLS], U16, name="offsets")
-        word_pool = keep.tile([P, T], I32, name="word_pool", align_bytes=64)
-        scale_pool = keep.tile([P, T // 4], I32, name="scale_pool", tag="late", align_bytes=64)
-        key_scales = keep.tile([P, B * N], U8, name="key_scales", align_bytes=64)
-        moved_scales = keep.tile([P, PASSES, B * N // 4], I32, name="moved_scales", align_bytes=64)
+        word_pool = keep.tile([P, T], I32, name="word_pool", align_bytes=256)
+        scale_pool = keep.tile([P, T // 4], I32, name="scale_pool", tag="late", align_bytes=256)
+        key_scales = keep.tile([P, B * N], U8, name="key_scales", align_bytes=256)
+        moved_scales = keep.tile([P, PASSES, B * N // 4], I32, name="moved_scales", align_bytes=256)
 
         nc.vector.memset(scale_pool[0:SCALE_BASE, :], 0)
         nc.vector.memset(moved_scales[:], 0)
 
         words_hbm = k_words[0].rearrange("p t c -> p (t c)").bitcast(I32)
         scales_hbm = k_scales.bitcast(I32)
-        nc.sync.dma_start(scale_pool[SCALE_BASE:P, :], scales_hbm.rearrange("o f w -> f o w"))
+        nc.scalar.dma_start(scale_pool[SCALE_BASE:P, :], scales_hbm.rearrange("o f w -> f o w"))
         nc.sync.dma_start(offsets[:], offs)
         q_raw = {}
 
@@ -57,24 +57,24 @@ def tile_attend_gumbel_seg_kernel(tc, qT, k_words, k_scales, gn, offs, out):
             nc.sync.dma_start(q_raw[b, o][:], qT[b].rearrange("(o p j) q -> o p j q", o=PASSES, j=PACK)[o])
 
         nc.sync.dma_start(word_pool[:, 0:SEG], words_hbm[:, 0:SEG])
-        load_queries(0, 0, keep.tile([P, PACK, NQ], F32, name="q_raw0_0", tag="noise", align_bytes=64))
-        load_queries(0, 1, shared.tile([P, PACK, NQ], F32, name="q_raw0_1", offset=PASS_BYTES, align_bytes=64))
+        load_queries(0, 0, keep.tile([P, PACK, NQ], F32, name="q_raw0_0", tag="noise", align_bytes=256))
+        load_queries(0, 1, shared.tile([P, PACK, NQ], F32, name="q_raw0_1", offset=PASS_BYTES, align_bytes=256))
         nc.sync.dma_start(word_pool[:, SEG:T], words_hbm[:, SEG:T])
-        load_queries(1, 0, third.tile([P, PACK, NQ], F32, name="q_raw1_0", offset=0, align_bytes=64))
+        load_queries(1, 0, third.tile([P, PACK, NQ], F32, name="q_raw1_0", offset=0, align_bytes=256))
 
         pairs = [
-            keep.tile([P, N], U32, name="pairs0", align_bytes=64),
-            shared.tile([P, N], U32, name="pairs1", offset=PASSES * PASS_BYTES, align_bytes=64),
+            keep.tile([P, N], U32, name="pairs0", align_bytes=256),
+            shared.tile([P, N], U32, name="pairs1", offset=PASSES * PASS_BYTES, align_bytes=256),
         ]
-        first_keys = shared.tile([P, PASSES, PASS_BYTES], U8, name="first_keys", offset=0, align_bytes=64)
-        last_keys = [third.tile([P, PASS_BYTES], U8, name="last_keys%d" % o, offset=PASS_BYTES * o, align_bytes=64) for o in range(PASSES)]
+        first_keys = shared.tile([P, PASSES, PASS_BYTES], U8, name="first_keys", offset=0, align_bytes=256)
+        last_keys = [third.tile([P, PASS_BYTES], U8, name="last_keys%d" % o, offset=PASS_BYTES * o, align_bytes=256) for o in range(PASSES)]
         key_words = {}
         for o in range(PASSES):
             key_words[0, o] = first_keys[:, o, :]
             key_words[1, o] = last_keys[o][:]
-        q_bf = [keep.tile([P, PASSES, NQ, PACK], BF16, name="q_bf%d" % b, align_bytes=64) for b in range(B)]
-        q_codes = [keep.tile([P, PASSES * NQ], U32, name="q_codes%d" % b, align_bytes=64) for b in range(B)]
-        q_scales = [keep.tile([P, PASSES * NQ], U8, name="q_scales%d" % b, align_bytes=64) for b in range(B)]
+        q_bf = [keep.tile([P, PASSES, NQ, PACK], BF16, name="q_bf%d" % b, align_bytes=256) for b in range(B)]
+        q_codes = [keep.tile([P, PASSES * NQ], U32, name="q_codes%d" % b, align_bytes=256) for b in range(B)]
+        q_scales = [keep.tile([P, PASSES * NQ], U8, name="q_scales%d" % b, align_bytes=256) for b in range(B)]
         scores = [psum.tile([P, N], F32, name=name) for name in ("first_scores", "last_scores")]
         by_pass = [pairs[b][:].bitcast(U16).rearrange("p (n o) -> p o n", o=PASSES) for b in range(B)]
 
@@ -112,16 +112,16 @@ def tile_attend_gumbel_seg_kernel(tc, qT, k_words, k_scales, gn, offs, out):
         nc.vector.tensor_copy(key_scales[:], scale_pool[:].bitcast(U8).indirect(offsets[:]))
         gathered = key_scales[:].bitcast(I32)
         rows_moved = BLOCK_ROWS * PASSES
-        for quadrant in range(QUADRANTS):
+        for quadrant in (0, 2, 1, 3):
             nc.sync.dma_start(
                 moved_scales[QUADRANT * quadrant : QUADRANT * quadrant + BLOCK_ROWS, :, :],
                 gathered[SCALE_BASE + rows_moved * quadrant : SCALE_BASE + rows_moved * (quadrant + 1), :],
             )
 
-        load_queries(1, 1, keep.tile([P, PACK, NQ], F32, name="q_raw1_1", tag="late", align_bytes=64))
+        load_queries(1, 1, keep.tile([P, PACK, NQ], F32, name="q_raw1_1", tag="late", align_bytes=256))
         gather_words(0)
         round_queries(0)
-        noise = keep.tile([P, B, N], F32, name="noise", tag="noise", align_bytes=64)
+        noise = keep.tile([P, B, N], F32, name="noise", tag="noise", align_bytes=256)
         for b in range(B):
             nc.sync.dma_start(noise[:, b, :], gn[b])
         round_queries(1)
@@ -136,15 +136,15 @@ def tile_attend_gumbel_seg_kernel(tc, qT, k_words, k_scales, gn, offs, out):
         quantise_queries(1, slice(1, 2))
         multiply(1)
 
-        first_sums = keep.tile([P, N], F32, name="first_sums", tag="late", align_bytes=64)
+        first_sums = keep.tile([P, N], F32, name="first_sums", tag="late", align_bytes=256)
         noisy = [first_sums[:], noise[:, 0, :]]
-        neg2 = [keep.tile([P, N], F32, name="neg2_%d" % b, align_bytes=64) for b in range(B)]
+        neg2 = [keep.tile([P, N], F32, name="neg2_%d" % b, align_bytes=256) for b in range(B)]
         part_shift = keep.tile([P, 1], F32, name="part_shift")
-        shift = [third.tile([P, 1], F32, name="shift0", offset=PASS_BYTES, align_bytes=64), keep.tile([P, 1], F32, name="shift1")]
-        expd = [keep.tile([P, N], F32, name="expd%d" % b, align_bytes=64) for b in range(B)]
+        shift = [third.tile([P, 1], F32, name="shift0", offset=PASS_BYTES, align_bytes=256), keep.tile([P, 1], F32, name="shift1")]
+        expd = [keep.tile([P, N], F32, name="expd%d" % b, align_bytes=256) for b in range(B)]
         total = [keep.tile([P, 1], F32, name="total%d" % b) for b in range(B)]
         inverse = [keep.tile([P, 1], F32, name="inverse%d" % b) for b in range(B)]
-        result = [keep.tile([P, N], F32, name="result%d" % b, align_bytes=64) for b in range(B)]
+        result = [keep.tile([P, N], F32, name="result%d" % b, align_bytes=256) for b in range(B)]
 
         def add_noise(b, cols):
             nc.vector.tensor_tensor(noisy[b][:, cols], scores[b][:, cols], noise[:, b, cols], ALU.add)

@@ -48,7 +48,7 @@ def tile_attend_gumbel_seg_kernel(tc, qT, k_words, k_scales, gn, offs, out):
 
         words_hbm = k_words[0].rearrange("p t c -> p (t c)").bitcast(I32)
         scales_hbm = k_scales.bitcast(I32)
-        nc.scalar.dma_start(scale_pool[SCALE_BASE:P, :], scales_hbm.rearrange("o f w -> f o w"))
+        nc.sync.dma_start(scale_pool[SCALE_BASE:P, :], scales_hbm.rearrange("o f w -> f o w"))
         nc.sync.dma_start(offsets[:], offs)
         q_raw = {}
 

@@ -112,7 +112,7 @@ def tile_attend_gumbel_seg_kernel(tc, qT, k_words, k_scales, gn, offs, out):
         nc.vector.tensor_copy(key_scales[:], scale_pool[:].bitcast(U8).indirect(offsets[:]))
         gathered = key_scales[:].bitcast(I32)
         rows_moved = BLOCK_ROWS * PASSES
-        for quadrant in (0, 2, 1, 3):
+        for quadrant in range(QUADRANTS):
             nc.sync.dma_start(
                 moved_scales[QUADRANT * quadrant : QUADRANT * quadrant + BLOCK_ROWS, :, :],
                 gathered[SCALE_BASE + rows_moved * quadrant : SCALE_BASE + rows_moved * (quadrant + 1), :],

@@ -27,6 +27,7 @@ BLOCK_ROWS = 4
 SCALE_BASE = P - QUADRANT
 PASS_BYTES = 2 * N
 EARLY = 384
+HALF = N // 2
 
 
 def tile_attend_gumbel_seg_kernel(tc, qT, k_words, k_scales, gn, offs, out):
@@ -75,7 +76,8 @@ def tile_attend_gumbel_seg_kernel(tc, qT, k_words, k_scales, gn, offs, out):
         q_bf = [keep.tile([P, PASSES, NQ, PACK], BF16, name="q_bf%d" % b, align_bytes=256) for b in range(B)]
         q_codes = [keep.tile([P, PASSES * NQ], U32, name="q_codes%d" % b, align_bytes=256) for b in range(B)]
         q_scales = [keep.tile([P, PASSES * NQ], U8, name="q_scales%d" % b, align_bytes=256) for b in range(B)]
-        scores = [psum.tile([P, N], F32, name=name) for name in ("first_scores", "last_scores")]
+        first_scores = psum.tile([P, N], F32, name="first_scores")
+        last_scores = [psum.tile([P, HALF], F32, name="last_scores%d" % h) for h in range(2)]
         by_pass = [pairs[b][:].bitcast(U16).rearrange("p (n o) -> p o n", o=PASSES) for b in range(B)]
 
         def gather_words(b):
@@ -97,17 +99,16 @@ def tile_attend_gumbel_seg_kernel(tc, qT, k_words, k_scales, gn, offs, out):
                 in_=q_bf[b][:, passes, :, :].rearrange("p o q j -> p (o q j)"),
             )
 
-        def multiply(b):
-            for o in range(PASSES):
-                nc.tensor.matmul_mx(
-                    out=scores[b][:],
-                    lhsT=q_codes[b][:, o * NQ : (o + 1) * NQ].bitcast(FP8X4),
-                    lhsT_scale=q_scales[b][:, o * NQ : (o + 1) * NQ],
-                    rhs=key_words[b, o].bitcast(FP4X4),
-                    rhs_scale=moved_scales[:, o, :].bitcast(U8)[:, b * N : (b + 1) * N],
-                    start=(o == 0),
-                    stop=(o == PASSES - 1),
-                )
+        def multiply(b, o, bank, cols):
+            nc.tensor.matmul_mx(
+                out=bank,
+                lhsT=q_codes[b][:, o * NQ : (o + 1) * NQ].bitcast(FP8X4),
+                lhsT_scale=q_scales[b][:, o * NQ : (o + 1) * NQ],
+                rhs=key_words[b, o][:, 2 * cols.start : 2 * cols.stop].bitcast(FP4X4),
+                rhs_scale=moved_scales[:, o, :].bitcast(U8)[:, b * N + cols.start : b * N + cols.stop],
+                start=(o == 0),
+                stop=(o == PASSES - 1),
+            )
 
         nc.vector.tensor_copy(key_scales[:], scale_pool[:].bitcast(U8).indirect(offsets[:]))
         gathered = key_scales[:].bitcast(I32)
@@ -128,13 +129,17 @@ def tile_attend_gumbel_seg_kernel(tc, qT, k_words, k_scales, gn, offs, out):
 
         quantise_queries(0, slice(0, PASSES))
         nc.vector.tensor_copy(first_keys[:].bitcast(U16), by_pass[0])
-        multiply(0)
+        for o in range(PASSES):
+            multiply(0, o, first_scores[:], slice(0, N))
         gather_words(1)
         quantise_queries(1, slice(0, 1))
         for o in range(PASSES):
             nc.vector.tensor_copy(last_keys[o][:].bitcast(U16), by_pass[1][:, o, :])
         quantise_queries(1, slice(1, 2))
-        multiply(1)
+        halves = [slice(0, HALF), slice(HALF, N)]
+        for o in range(PASSES):
+            for h in range(2):
+                multiply(1, o, last_scores[h][:], halves[h])
 
         first_sums = keep.tile([P, N], F32, name="first_sums", tag="late", align_bytes=256)
         noisy = [first_sums[:], noise[:, 0, :]]
@@ -146,8 +151,8 @@ def tile_attend_gumbel_seg_kernel(tc, qT, k_words, k_scales, gn, offs, out):
         inverse = [keep.tile([P, 1], F32, name="inverse%d" % b) for b in range(B)]
         result = [keep.tile([P, N], F32, name="result%d" % b, align_bytes=256) for b in range(B)]
 
-        def add_noise(b, cols):
-            nc.vector.tensor_tensor(noisy[b][:, cols], scores[b][:, cols], noise[:, b, cols], ALU.add)
+        def add_noise(b, cols, scores):
+            nc.vector.tensor_tensor(noisy[b][:, cols], scores, noise[:, b, cols], ALU.add)
 
         def row_minimum(b, cols, start, target):
             nc.vector.tensor_scalar(neg2[b][:, cols], noisy[b][:, cols], -2.0, start, ALU.mult, ALU.min, accum_out=target)
@@ -156,10 +161,11 @@ def tile_attend_gumbel_seg_kernel(tc, qT, k_words, k_scales, gn, offs, out):
             nc.scalar.activation(expd[b][:], neg2[b][:], ACT.Exp, bias=shift[b][:], scale=-1.0, accum_out=total[b][:])
 
         early, late, whole = slice(0, EARLY), slice(EARLY, N), slice(0, N)
-        add_noise(0, early)
-        add_noise(0, late)
+        add_noise(0, early, first_scores[:, early])
+        add_noise(0, late, first_scores[:, late])
         row_minimum(0, early, None, part_shift[:])
-        add_noise(1, whole)
+        for h in range(2):
+            add_noise(1, halves[h], last_scores[h][:])
         row_minimum(0, late, part_shift[:], shift[0][:])
         exponentials(0)
         row_minimum(1, whole, None, shift[1][:])

@@ -20,76 +20,73 @@ P = 128
 PACK = 4
 PASSES = D // (P * PACK)
 SEG = T // B
-LIST_COLS = N // 16
 QUADRANT = 32
 QUADRANTS = P // QUADRANT
 BLOCK_ROWS = 4
 SCALE_BASE = P - QUADRANT
-PASS_BYTES = 2 * N
-EARLY = 384
 HALF = N // 2
+KB = 1024
+EARLY = 384
 
 
 def tile_attend_gumbel_seg_kernel(tc, qT, k_words, k_scales, gn, offs, out):
     nc = tc.nc
     with ExitStack() as ctx:
         keep = ctx.enter_context(tc.tile_pool(name="keep", bufs=1))
-        shared = ctx.enter_context(tc.tile_pool(name="shared", bufs=1))
+        first = ctx.enter_context(tc.tile_pool(name="first", bufs=1))
+        second = ctx.enter_context(tc.tile_pool(name="second", bufs=1))
         third = ctx.enter_context(tc.tile_pool(name="third", bufs=1))
         psum = ctx.enter_context(tc.psum_pool(name="psum", bufs=1))
 
-        offsets = keep.tile([P, B * LIST_COLS], U16, name="offsets")
+        offsets = keep.tile([P, B * N // 16], U16, name="offsets")
         word_pool = keep.tile([P, T], I32, name="word_pool", align_bytes=256)
-        scale_pool = keep.tile([P, T // 4], I32, name="scale_pool", tag="late", align_bytes=256)
+        scale_pool = keep.tile([P, T // 4], I32, name="scale_pool", align_bytes=256)
         key_scales = keep.tile([P, B * N], U8, name="key_scales", align_bytes=256)
         moved_scales = keep.tile([P, PASSES, B * N // 4], I32, name="moved_scales", align_bytes=256)
-
         nc.vector.memset(scale_pool[0:SCALE_BASE, :], 0)
         nc.vector.memset(moved_scales[:], 0)
 
         words_hbm = k_words[0].rearrange("p t c -> p (t c)").bitcast(I32)
-        scales_hbm = k_scales.bitcast(I32)
-        nc.sync.dma_start(scale_pool[SCALE_BASE:P, :], scales_hbm.rearrange("o f w -> f o w"))
+        nc.sync.dma_start(scale_pool[SCALE_BASE:P, :], k_scales.bitcast(I32).rearrange("o f w -> f o w"))
         nc.sync.dma_start(offsets[:], offs)
         q_raw = {}
 
-        def load_queries(b, o, tile):
-            q_raw[b, o] = tile
-            nc.sync.dma_start(q_raw[b, o][:], qT[b].rearrange("(o p j) q -> o p j q", o=PASSES, j=PACK)[o])
+        def load_queries(b, o, tile, queue):
+            q_raw[b, o] = tile[:, 0:PACK, :]
+            queue.dma_start(q_raw[b, o], qT[b].rearrange("(o p j) q -> o p j q", o=PASSES, j=PACK)[o])
 
         nc.sync.dma_start(word_pool[:, 0:SEG], words_hbm[:, 0:SEG])
-        load_queries(0, 0, keep.tile([P, PACK, NQ], F32, name="q_raw0_0", tag="noise", align_bytes=256))
-        load_queries(0, 1, shared.tile([P, PACK, NQ], F32, name="q_raw0_1", offset=PASS_BYTES, align_bytes=256))
+        load_queries(0, 0, third.tile([P, PACK, NQ], F32, name="q_raw0_0", offset=3 * KB, align_bytes=256), nc.sync)
+        load_queries(0, 1, first.tile([P, PACK, NQ], F32, name="q_raw0_1", offset=KB, align_bytes=256), nc.sync)
         nc.sync.dma_start(word_pool[:, SEG:T], words_hbm[:, SEG:T])
-        load_queries(1, 0, third.tile([P, PACK, NQ], F32, name="q_raw1_0", offset=0, align_bytes=256))
+        load_queries(1, 0, second.tile([P, PACK, NQ], F32, name="q_raw1_0", offset=0, align_bytes=256), nc.sync)
 
-        pairs = [
-            keep.tile([P, N], U32, name="pairs0", align_bytes=256),
-            shared.tile([P, N], U32, name="pairs1", offset=PASSES * PASS_BYTES, align_bytes=256),
+        first_pairs = keep.tile([P, N], U32, name="first_pairs", align_bytes=256)
+        first_keys = first.tile([P, PASSES, 2 * N], U8, name="first_keys", offset=0, align_bytes=256)
+        half_pairs = [
+            first.tile([P, HALF], U32, name="half_pairs0", offset=2 * KB, align_bytes=256),
+            second.tile([P, HALF], U32, name="half_pairs1", offset=KB, align_bytes=256),
         ]
-        first_keys = shared.tile([P, PASSES, PASS_BYTES], U8, name="first_keys", offset=0, align_bytes=256)
-        last_keys = [third.tile([P, PASS_BYTES], U8, name="last_keys%d" % o, offset=PASS_BYTES * o, align_bytes=256) for o in range(PASSES)]
-        key_words = {}
-        for o in range(PASSES):
-            key_words[0, o] = first_keys[:, o, :]
-            key_words[1, o] = last_keys[o][:]
+        early_keys = second.tile([P, PASSES, 2 * HALF], U8, name="early_keys", offset=0, align_bytes=256)
         q_bf = [keep.tile([P, PASSES, NQ, PACK], BF16, name="q_bf%d" % b, align_bytes=256) for b in range(B)]
         q_codes = [keep.tile([P, PASSES * NQ], U32, name="q_codes%d" % b, align_bytes=256) for b in range(B)]
         q_scales = [keep.tile([P, PASSES * NQ], U8, name="q_scales%d" % b, align_bytes=256) for b in range(B)]
         first_scores = psum.tile([P, N], F32, name="first_scores")
-        last_scores = [psum.tile([P, HALF], F32, name="last_scores%d" % h) for h in range(2)]
-        by_pass = [pairs[b][:].bitcast(U16).rearrange("p (n o) -> p o n", o=PASSES) for b in range(B)]
+        half_scores = [psum.tile([P, HALF], F32, name="half_scores%d" % h) for h in range(2)]
 
-        def gather_words(b):
+        def gather_words(pairs, b, slots):
             window = word_pool[:, 0 : (b + 1) * SEG].bitcast(U32)
-            nc.vector.tensor_copy(pairs[b][:], window.indirect(offsets[:, b * LIST_COLS : (b + 1) * LIST_COLS]))
+            entries = slice((b * N + slots.start) // 16, (b * N + slots.stop) // 16)
+            nc.vector.tensor_copy(pairs[:], window.indirect(offsets[:, entries]))
 
-        def round_queries(b):
-            for o in range(PASSES):
-                nc.scalar.copy(
-                    q_bf[b][:, o, :, :].rearrange("p (c i) j -> p c j i", i=4),
-                    q_raw[b, o][:].rearrange("p j (c i) -> p c j i", i=4),
-                )
+        def by_pass(pairs):
+            return pairs[:].bitcast(U16).rearrange("p (n o) -> p o n", o=PASSES)
+
+        def round_queries(b, o):
+            nc.scalar.copy(
+                q_bf[b][:, o, :, :].rearrange("p (c i) j -> p c j i", i=4),
+                q_raw[b, o].rearrange("p j (c i) -> p c j i", i=4),
+            )
 
         def quantise_queries(b, passes):
             cols = slice(passes.start * NQ, passes.stop * NQ)
@@ -99,13 +96,13 @@ def tile_attend_gumbel_seg_kernel(tc, qT, k_words, k_scales, gn, offs, out):
                 in_=q_bf[b][:, passes, :, :].rearrange("p o q j -> p (o q j)"),
             )
 
-        def multiply(b, o, bank, cols):
+        def multiply(bank, b, o, keys, slots):
             nc.tensor.matmul_mx(
-                out=bank,
+                out=bank[:],
                 lhsT=q_codes[b][:, o * NQ : (o + 1) * NQ].bitcast(FP8X4),
                 lhsT_scale=q_scales[b][:, o * NQ : (o + 1) * NQ],
-                rhs=key_words[b, o][:, 2 * cols.start : 2 * cols.stop].bitcast(FP4X4),
-                rhs_scale=moved_scales[:, o, :].bitcast(U8)[:, b * N + cols.start : b * N + cols.stop],
+                rhs=keys.bitcast(FP4X4),
+                rhs_scale=moved_scales[:, o, :].bitcast(U8)[:, b * N + slots.start : b * N + slots.stop],
                 start=(o == 0),
                 stop=(o == PASSES - 1),
             )
@@ -119,33 +116,39 @@ def tile_attend_gumbel_seg_kernel(tc, qT, k_words, k_scales, gn, offs, out):
                 gathered[SCALE_BASE + rows_moved * quadrant : SCALE_BASE + rows_moved * (quadrant + 1), :],
             )
 
-        load_queries(1, 1, keep.tile([P, PACK, NQ], F32, name="q_raw1_1", tag="late", align_bytes=256))
-        gather_words(0)
-        round_queries(0)
-        noise = keep.tile([P, B, N], F32, name="noise", tag="noise", align_bytes=256)
+        whole, halves = slice(0, N), [slice(0, HALF), slice(HALF, N)]
+        gather_words(first_pairs, 0, whole)
+        round_queries(0, 0)
+        load_queries(1, 1, third.tile([P, 2 * PACK, NQ], F32, name="q_raw1_1", offset=0, align_bytes=256), nc.scalar)
+        round_queries(0, 1)
+        noise = third.tile([P, B, N], F32, name="noise", offset=4 * KB, align_bytes=256)
         for b in range(B):
             nc.sync.dma_start(noise[:, b, :], gn[b])
-        round_queries(1)
+        for o in range(PASSES):
+            round_queries(1, o)
 
         quantise_queries(0, slice(0, PASSES))
-        nc.vector.tensor_copy(first_keys[:].bitcast(U16), by_pass[0])
+        nc.vector.tensor_copy(first_keys[:].bitcast(U16), by_pass(first_pairs))
         for o in range(PASSES):
-            multiply(0, o, first_scores[:], slice(0, N))
-        gather_words(1)
+            multiply(first_scores, 0, o, first_keys[:, o, :], whole)
+        gather_words(half_pairs[0], 1, halves[0])
         quantise_queries(1, slice(0, 1))
-        for o in range(PASSES):
-            nc.vector.tensor_copy(last_keys[o][:].bitcast(U16), by_pass[1][:, o, :])
+        nc.vector.tensor_copy(early_keys[:].bitcast(U16), by_pass(half_pairs[0]))
+        gather_words(half_pairs[1], 1, halves[1])
         quantise_queries(1, slice(1, 2))
-        halves = [slice(0, HALF), slice(HALF, N)]
         for o in range(PASSES):
-            for h in range(2):
-                multiply(1, o, last_scores[h][:], halves[h])
+            multiply(half_scores[0], 1, o, early_keys[:, o, :], halves[0])
+        late_keys = third.tile([P, PASSES, 2 * HALF], U8, name="late_keys", offset=0, align_bytes=256)
+        nc.vector.tensor_copy(late_keys[:].bitcast(U16), by_pass(half_pairs[1]))
+        for o in range(PASSES):
+            multiply(half_scores[1], 1, o, late_keys[:, o, :], halves[1])
 
-        first_sums = keep.tile([P, N], F32, name="first_sums", tag="late", align_bytes=256)
-        noisy = [first_sums[:], noise[:, 0, :]]
+        first_sums = third.tile([P, N], F32, name="first_sums", offset=KB, align_bytes=256)
+        last_sums = keep.tile([P, N], F32, name="last_sums", align_bytes=256)
+        noisy = [first_sums[:], last_sums[:]]
         neg2 = [keep.tile([P, N], F32, name="neg2_%d" % b, align_bytes=256) for b in range(B)]
         part_shift = keep.tile([P, 1], F32, name="part_shift")
-        shift = [third.tile([P, 1], F32, name="shift0", offset=PASS_BYTES, align_bytes=256), keep.tile([P, 1], F32, name="shift1")]
+        shift = [keep.tile([P, 1], F32, name="shift%d" % b) for b in range(B)]
         expd = [keep.tile([P, N], F32, name="expd%d" % b, align_bytes=256) for b in range(B)]
         total = [keep.tile([P, 1], F32, name="total%d" % b) for b in range(B)]
         inverse = [keep.tile([P, 1], F32, name="inverse%d" % b) for b in range(B)]
@@ -160,12 +163,11 @@ def tile_attend_gumbel_seg_kernel(tc, qT, k_words, k_scales, gn, offs, out):
         def exponentials(b):
             nc.scalar.activation(expd[b][:], neg2[b][:], ACT.Exp, bias=shift[b][:], scale=-1.0, accum_out=total[b][:])
 
-        early, late, whole = slice(0, EARLY), slice(EARLY, N), slice(0, N)
-        add_noise(0, early, first_scores[:, early])
-        add_noise(0, late, first_scores[:, late])
+        early, late = slice(0, EARLY), slice(EARLY, N)
+        add_noise(0, whole, first_scores[:])
+        add_noise(1, halves[0], half_scores[0][:])
         row_minimum(0, early, None, part_shift[:])
-        for h in range(2):
-            add_noise(1, halves[h], last_scores[h][:])
+        add_noise(1, halves[1], half_scores[1][:])
         row_minimum(0, late, part_shift[:], shift[0][:])
         exponentials(0)
         row_minimum(1, whole, None, shift[1][:])

@@ -40,7 +40,7 @@ def tile_attend_gumbel_seg_kernel(tc, qT, k_words, k_scales, gn, offs, out):
 
         offsets = keep.tile([P, B * N // 16], U16, name="offsets")
         word_pool = keep.tile([P, T], I32, name="word_pool", align_bytes=256)
-        scale_pool = keep.tile([P, T // 4], I32, name="scale_pool", align_bytes=256)
+        scale_pool = third.tile([P, T // 4], I32, name="scale_pool", offset=0, align_bytes=256)
         key_scales = keep.tile([P, B * N], U8, name="key_scales", align_bytes=256)
         moved_scales = keep.tile([P, PASSES, B * N // 4], I32, name="moved_scales", align_bytes=256)
         nc.vector.memset(scale_pool[0:SCALE_BASE, :], 0)
@@ -56,7 +56,7 @@ def tile_attend_gumbel_seg_kernel(tc, qT, k_words, k_scales, gn, offs, out):
             queue.dma_start(q_raw[b, o], qT[b].rearrange("(o p j) q -> o p j q", o=PASSES, j=PACK)[o])
 
         nc.sync.dma_start(word_pool[:, 0:SEG], words_hbm[:, 0:SEG])
-        load_queries(0, 0, third.tile([P, PACK, NQ], F32, name="q_raw0_0", offset=3 * KB, align_bytes=256), nc.sync)
+        load_queries(0, 0, third.tile([P, PACK, NQ], F32, name="q_raw0_0", offset=4 * KB, align_bytes=256), nc.sync)
         load_queries(0, 1, first.tile([P, PACK, NQ], F32, name="q_raw0_1", offset=KB, align_bytes=256), nc.sync)
         nc.sync.dma_start(word_pool[:, SEG:T], words_hbm[:, SEG:T])
         load_queries(1, 0, second.tile([P, PACK, NQ], F32, name="q_raw1_0", offset=0, align_bytes=256), nc.sync)
@@ -119,7 +119,7 @@ def tile_attend_gumbel_seg_kernel(tc, qT, k_words, k_scales, gn, offs, out):
         whole, halves = slice(0, N), [slice(0, HALF), slice(HALF, N)]
         gather_words(first_pairs, 0, whole)
         round_queries(0, 0)
-        load_queries(1, 1, third.tile([P, 2 * PACK, NQ], F32, name="q_raw1_1", offset=0, align_bytes=256), nc.scalar)
+        load_queries(1, 1, third.tile([P, 2 * PACK, NQ], F32, name="q_raw1_1", offset=0, align_bytes=256), nc.sync)
         round_queries(0, 1)
         noise = third.tile([P, B, N], F32, name="noise", offset=4 * KB, align_bytes=256)
         for b in range(B):
@@ -135,17 +135,15 @@ def tile_attend_gumbel_seg_kernel(tc, qT, k_words, k_scales, gn, offs, out):
         quantise_queries(1, slice(0, 1))
         nc.vector.tensor_copy(early_keys[:].bitcast(U16), by_pass(half_pairs[0]))
         gather_words(half_pairs[1], 1, halves[1])
+        late_keys = keep.tile([P, PASSES, 2 * HALF], U8, name="late_keys", align_bytes=256)
+        nc.vector.tensor_copy(late_keys[:].bitcast(U16), by_pass(half_pairs[1]))
         quantise_queries(1, slice(1, 2))
         for o in range(PASSES):
-            multiply(half_scores[0], 1, o, early_keys[:, o, :], halves[0])
-        late_keys = third.tile([P, PASSES, 2 * HALF], U8, name="late_keys", offset=0, align_bytes=256)
-        nc.vector.tensor_copy(late_keys[:].bitcast(U16), by_pass(half_pairs[1]))
-        for o in range(PASSES):
-            multiply(half_scores[1], 1, o, late_keys[:, o, :], halves[1])
+            for h, keys in enumerate((early_keys, late_keys)):
+                multiply(half_scores[h], 1, o, keys[:, o, :], halves[h])
 
         first_sums = third.tile([P, N], F32, name="first_sums", offset=KB, align_bytes=256)
-        last_sums = keep.tile([P, N], F32, name="last_sums", align_bytes=256)
-        noisy = [first_sums[:], last_sums[:]]
+        noisy = [first_sums[:], noise[:, 0, :]]
         neg2 = [keep.tile([P, N], F32, name="neg2_%d" % b, align_bytes=256) for b in range(B)]
         part_shift = keep.tile([P, 1], F32, name="part_shift")
         shift = [keep.tile([P, 1], F32, name="shift%d" % b) for b in range(B)]
@@ -164,10 +162,11 @@ def tile_attend_gumbel_seg_kernel(tc, qT, k_words, k_scales, gn, offs, out):
             nc.scalar.activation(expd[b][:], neg2[b][:], ACT.Exp, bias=shift[b][:], scale=-1.0, accum_out=total[b][:])
 
         early, late = slice(0, EARLY), slice(EARLY, N)
-        add_noise(0, whole, first_scores[:])
-        add_noise(1, halves[0], half_scores[0][:])
+        add_noise(0, early, first_scores[:, early])
+        add_noise(0, late, first_scores[:, late])
         row_minimum(0, early, None, part_shift[:])
-        add_noise(1, halves[1], half_scores[1][:])
+        for h in range(2):
+            add_noise(1, halves[h], half_scores[h][:])
         row_minimum(0, late, part_shift[:], shift[0][:])
         exponentials(0)
         row_minimum(1, whole, None, shift[1][:])

@@ -133,8 +133,8 @@ def tile_attend_gumbel_seg_kernel(tc, qT, k_words, k_scales, gn, offs, out):
             multiply(first_scores, 0, o, first_keys[:, o, :], whole)
         gather_words(half_pairs[0], 1, halves[0])
         quantise_queries(1, slice(0, 1))
-        nc.vector.tensor_copy(early_keys[:].bitcast(U16), by_pass(half_pairs[0]))
         gather_words(half_pairs[1], 1, halves[1])
+        nc.vector.tensor_copy(early_keys[:].bitcast(U16), by_pass(half_pairs[0]))
         late_keys = keep.tile([P, PASSES, 2 * HALF], U8, name="late_keys", align_bytes=256)
         nc.vector.tensor_copy(late_keys[:].bitcast(U16), by_pass(half_pairs[1]))
         quantise_queries(1, slice(1, 2))

from contextlib import ExitStack

import concourse.mybir as mybir

B, N, T, D, NQ = 2, 512, 2048, 1024, 128
FLOPS = 2 * B * NQ * N * D

F32 = mybir.dt.float32
BF16 = mybir.dt.bfloat16
I32 = mybir.dt.int32
U32 = mybir.dt.uint32
U16 = mybir.dt.uint16
U8 = mybir.dt.uint8
FP8X4 = mybir.dt.float8_e4m3fn_x4
FP4X4 = mybir.dt.float4_e2m1fn_x4
ALU = mybir.AluOpType
ACT = mybir.ActivationFunctionType

P = 128
PACK = 4
PASSES = D // (P * PACK)
SEG = T // B
QUADRANT = 32
QUADRANTS = P // QUADRANT
BLOCK_ROWS = 4
SCALE_BASE = P - QUADRANT
HALF = N // 2
KB = 1024
EARLY = 384


def tile_attend_gumbel_seg_kernel(tc, qT, k_words, k_scales, gn, offs, out):
    nc = tc.nc
    with ExitStack() as ctx:
        keep = ctx.enter_context(tc.tile_pool(name="keep", bufs=1))
        first = ctx.enter_context(tc.tile_pool(name="first", bufs=1))
        second = ctx.enter_context(tc.tile_pool(name="second", bufs=1))
        third = ctx.enter_context(tc.tile_pool(name="third", bufs=1))
        psum = ctx.enter_context(tc.psum_pool(name="psum", bufs=1))

        offsets = keep.tile([P, B * N // 16], U16, name="offsets")
        word_pool = keep.tile([P, T], I32, name="word_pool", align_bytes=256)
        scale_pool = third.tile([P, T // 4], I32, name="scale_pool", offset=0, align_bytes=256)
        key_scales = keep.tile([P, B * N], U8, name="key_scales", align_bytes=256)
        moved_scales = keep.tile([P, PASSES, B * N // 4], I32, name="moved_scales", align_bytes=256)
        nc.vector.memset(scale_pool[0:SCALE_BASE, :], 0)
        nc.vector.memset(moved_scales[:], 0)

        words_hbm = k_words[0].rearrange("p t c -> p (t c)").bitcast(I32)
        nc.sync.dma_start(scale_pool[SCALE_BASE:P, :], k_scales.bitcast(I32).rearrange("o f w -> f o w"))
        nc.sync.dma_start(offsets[:], offs)
        q_raw = {}

        def load_queries(b, o, tile, queue):
            q_raw[b, o] = tile[:, 0:PACK, :]
            queue.dma_start(q_raw[b, o], qT[b].rearrange("(o p j) q -> o p j q", o=PASSES, j=PACK)[o])

        nc.sync.dma_start(word_pool[:, 0:SEG], words_hbm[:, 0:SEG])
        load_queries(0, 0, third.tile([P, PACK, NQ], F32, name="q_raw0_0", offset=4 * KB, align_bytes=256), nc.sync)
        load_queries(0, 1, first.tile([P, PACK, NQ], F32, name="q_raw0_1", offset=KB, align_bytes=256), nc.sync)
        nc.sync.dma_start(word_pool[:, SEG:T], words_hbm[:, SEG:T])
        load_queries(1, 0, second.tile([P, PACK, NQ], F32, name="q_raw1_0", offset=0, align_bytes=256), nc.sync)

        first_pairs = keep.tile([P, N], U32, name="first_pairs", align_bytes=256)
        first_keys = first.tile([P, PASSES, 2 * N], U8, name="first_keys", offset=0, align_bytes=256)
        half_pairs = [
            first.tile([P, HALF], U32, name="half_pairs0", offset=2 * KB, align_bytes=256),
            second.tile([P, HALF], U32, name="half_pairs1", offset=KB, align_bytes=256),
        ]
        early_keys = second.tile([P, PASSES, 2 * HALF], U8, name="early_keys", offset=0, align_bytes=256)
        q_bf = [keep.tile([P, PASSES, NQ, PACK], BF16, name="q_bf%d" % b, align_bytes=256) for b in range(B)]
        q_codes = [keep.tile([P, PASSES * NQ], U32, name="q_codes%d" % b, align_bytes=256) for b in range(B)]
        q_scales = [keep.tile([P, PASSES * NQ], U8, name="q_scales%d" % b, align_bytes=256) for b in range(B)]
        first_scores = psum.tile([P, N], F32, name="first_scores")
        half_scores = [psum.tile([P, HALF], F32, name="half_scores%d" % h) for h in range(2)]

        def gather_words(pairs, b, slots):
            window = word_pool[:, 0 : (b + 1) * SEG].bitcast(U32)
            entries = slice((b * N + slots.start) // 16, (b * N + slots.stop) // 16)
            nc.vector.tensor_copy(pairs[:], window.indirect(offsets[:, entries]))

        def by_pass(pairs):
            return pairs[:].bitcast(U16).rearrange("p (n o) -> p o n", o=PASSES)

        def round_queries(b, o):
            nc.scalar.copy(
                q_bf[b][:, o, :, :].rearrange("p (c i) j -> p c j i", i=4),
                q_raw[b, o].rearrange("p j (c i) -> p c j i", i=4),
            )

        def quantise_queries(b, passes):
            cols = slice(passes.start * NQ, passes.stop * NQ)
            nc.vector.quantize_mx(
                out=q_codes[b][:, cols].bitcast(FP8X4),
                scales=q_scales[b][:, cols],
                in_=q_bf[b][:, passes, :, :].rearrange("p o q j -> p (o q j)"),
            )

        def multiply(bank, b, o, keys, slots):
            nc.tensor.matmul_mx(
                out=bank[:],
                lhsT=q_codes[b][:, o * NQ : (o + 1) * NQ].bitcast(FP8X4),
                lhsT_scale=q_scales[b][:, o * NQ : (o + 1) * NQ],
                rhs=keys.bitcast(FP4X4),
                rhs_scale=moved_scales[:, o, :].bitcast(U8)[:, b * N + slots.start : b * N + slots.stop],
                start=(o == 0),
                stop=(o == PASSES - 1),
            )

        nc.vector.tensor_copy(key_scales[:], scale_pool[:].bitcast(U8).indirect(offsets[:]))
        gathered = key_scales[:].bitcast(I32)
        rows_moved = BLOCK_ROWS * PASSES
        for quadrant in range(QUADRANTS):
            nc.sync.dma_start(
                moved_scales[QUADRANT * quadrant : QUADRANT * quadrant + BLOCK_ROWS, :, :],
                gathered[SCALE_BASE + rows_moved * quadrant : SCALE_BASE + rows_moved * (quadrant + 1), :],
            )

        whole, halves = slice(0, N), [slice(0, HALF), slice(HALF, N)]
        gather_words(first_pairs, 0, whole)
        round_queries(0, 0)
        load_queries(1, 1, third.tile([P, 2 * PACK, NQ], F32, name="q_raw1_1", offset=0, align_bytes=256), nc.sync)
        round_queries(0, 1)
        noise = third.tile([P, B, N], F32, name="noise", offset=4 * KB, align_bytes=256)
        for b in range(B):
            nc.sync.dma_start(noise[:, b, :], gn[b])
        for o in range(PASSES):
            round_queries(1, o)

        quantise_queries(0, slice(0, PASSES))
        nc.vector.tensor_copy(first_keys[:].bitcast(U16), by_pass(first_pairs))
        for o in range(PASSES):
            multiply(first_scores, 0, o, first_keys[:, o, :], whole)
        gather_words(half_pairs[0], 1, halves[0])
        quantise_queries(1, slice(0, 1))
        gather_words(half_pairs[1], 1, halves[1])
        nc.vector.tensor_copy(early_keys[:].bitcast(U16), by_pass(half_pairs[0]))
        late_keys = keep.tile([P, PASSES, 2 * HALF], U8, name="late_keys", align_bytes=256)
        nc.vector.tensor_copy(late_keys[:].bitcast(U16), by_pass(half_pairs[1]))
        quantise_queries(1, slice(1, 2))
        for o in range(PASSES):
            for h, keys in enumerate((early_keys, late_keys)):
                multiply(half_scores[h], 1, o, keys[:, o, :], halves[h])

        first_sums = third.tile([P, N], F32, name="first_sums", offset=KB, align_bytes=256)
        noisy = [first_sums[:], noise[:, 0, :]]
        neg2 = [keep.tile([P, N], F32, name="neg2_%d" % b, align_bytes=256) for b in range(B)]
        part_shift = keep.tile([P, 1], F32, name="part_shift")
        shift = [keep.tile([P, 1], F32, name="shift%d" % b) for b in range(B)]
        expd = [keep.tile([P, N], F32, name="expd%d" % b, align_bytes=256) for b in range(B)]
        total = [keep.tile([P, 1], F32, name="total%d" % b) for b in range(B)]
        inverse = [keep.tile([P, 1], F32, name="inverse%d" % b) for b in range(B)]
        result = [keep.tile([P, N], F32, name="result%d" % b, align_bytes=256) for b in range(B)]

        def add_noise(b, cols, scores):
            nc.vector.tensor_tensor(noisy[b][:, cols], scores, noise[:, b, cols], ALU.add)

        def row_minimum(b, cols, start, target):
            nc.vector.tensor_scalar(neg2[b][:, cols], noisy[b][:, cols], -2.0, start, ALU.mult, ALU.min, accum_out=target)

        def exponentials(b):
            nc.scalar.activation(expd[b][:], neg2[b][:], ACT.Exp, bias=shift[b][:], scale=-1.0, accum_out=total[b][:])

        early, late = slice(0, EARLY), slice(EARLY, N)
        add_noise(0, early, first_scores[:, early])
        add_noise(0, late, first_scores[:, late])
        row_minimum(0, early, None, part_shift[:])
        for h in range(2):
            add_noise(1, halves[h], half_scores[h][:])
        row_minimum(0, late, part_shift[:], shift[0][:])
        exponentials(0)
        row_minimum(1, whole, None, shift[1][:])
        exponentials(1)

        for b in range(B):
            nc.vector.reciprocal(inverse[b][:], total[b][:])
            queues = [nc.sync, nc.scalar] if b == B - 1 else [nc.sync]
            width = N // len(queues)
            for part, queue in enumerate(queues):
                cols = slice(part * width, (part + 1) * width)
                nc.vector.tensor_scalar(result[b][:, cols], expd[b][:, cols], inverse[b][:], None, ALU.mult)
                queue.dma_start(out[b, :, cols], result[b][:, cols])
